import numpy as np, ml_dtypes
CORES = [78,86,94,102,110,118]
N = 6
BF = ml_dtypes.bfloat16
V, TY, LN, SL, RT, RO, ST = 1024, 2048, 384, 48, 16, 4, 320
WT = 1 + 10 * np.arange(16)
def cand(u):
    return ((u * u >> 5) + u + np.arange(16)[:, None] * (2 * u + 1)) & (V - 1)
def pack(w, x, q, s, h, v, t):
    i = lambda a, n: np.ascontiguousarray(a).reshape(N, -1, n).astype(np.int32)
    b = lambda a, n: np.ascontiguousarray(a).reshape(N, -1, n).astype(np.float32).astype(BF)
    return {"wd": i(w, V), "xs": b(x, V), "rq": i(q, TY), "sg": b(s, TY), "hy": i(h, V), "vf": i(v, V), "th": i(t, 1)}
def world(rng, A, top, size, twin, noise, pw, wrong, harm):
    w = np.zeros((N, 8, 16, V), np.int64); x = w.copy(); q = np.zeros((N, 8, 16, TY), np.int64); s = q.copy(); h = np.zeros((N, 8, V), np.int64); tt = h.copy()
    for r in range(N):
        for g in range(8):
            live = rng.permutation(TY)[:A]
            sa = rng.integers(0, top + 1, (16, TY)) >> rng.integers(0, size + 1, (1, TY))
            sa[:, live[1::2]] = np.clip(sa[:, live[0::2]] + rng.integers(-twin, twin + 1, (16, A // 2)), 0, 255)
            qa = np.where(rng.random((16, TY)) < rng.random((1, TY)), live[(A * rng.random((16, TY)) ** pw).astype(np.int64)], TY)
            k = rng.permutation(np.concatenate([np.arange(A), (A * rng.random(V - A) ** pw).astype(np.int64)]))
            o = np.argsort(k, kind="stable"); n = np.bincount(k, minlength=A); b = np.add.accumulate(n) - n
            back = np.zeros(TY + 1, np.int64); back[live] = np.arange(A)
            need = qa[:, live[k]]; kk = back[need]
            wa = o[b[kk] + (n[kk] * rng.random((16, V)) ** pw).astype(np.int64)]
            p = rng.choice(np.array([0.0, 0.0, 0.0, 0.0, 0.0, 0.0, 0.15, 0.15, 0.15, 0.5]), V) * harm
            wa = np.where((need == TY) | (rng.random((16, V)) < p), rng.integers(0, V, (16, V)), wa)
            off = np.where(rng.random(V) < 0.5, live[rng.integers(0, A, V)], rng.integers(0, TY, V))
            h[r, g] = np.where(rng.random(V) < wrong[r, g], off, live[k]); tt[r, g] = live[k]
            x[r, g] = np.clip(sa[:, live[k]] + rng.integers(-noise, noise + 1, (16, V)), 0, 255)
            w[r, g], q[r, g], s[r, g] = wa, qa, sa
    return w, x, q, s, h, tt
def setup_inputs(rng):
    wrong = rng.choice(np.array([0.004, 0.02, 0.06, 0.15]), (N, 8))
    w, x, q, s, h, tt = world(rng, min(V, TY) // 2, 255, 0, 3, 4, 1, wrong, 1.0)
    v = rng.random((N, 8, V)) < rng.choice(np.array([0.02, 0.2, 0.5, 0.85]), (N, 8, 1))
    t = 40 + (1200 * rng.random((N, 8, 16)) ** 2).astype(np.int64)
    return pack(w, x, q, s, h, v, t)
def setup_inputs_spread(rng):
    w, x, q, s, h, tt = world(rng, min(V, TY) // 2, 255, 7, 2, 4, 3, 0.2 * rng.random((N, 8)), 1.0)
    v = rng.random((N, 8, V)) < rng.random((N, 8, 1))
    t = np.minimum(np.exp2(12 * rng.random((N, 8, 16))).astype(np.int64) - 1, 4080)
    return pack(w, x, q, s, h, v, t)
def setup_inputs_ties(rng):
    w, x, q, s, h, tt = world(rng, 8, 150, 0, 0, 0, 1, rng.choice(np.array([0.1, 0.3, 0.5]), (N, 8)), 0.5)
    near = np.array([49, 50, 51])
    x = np.take_along_axis(s, np.broadcast_to(tt[:, :, None, :], (N, 8, 16, V)), 3)
    x = x + (np.arange(16)[:, None] == rng.integers(0, 16, (N, 8, 1, V))) * rng.choice(near, (N, 8, 1, V))
    v = rng.random((N, 8, V)) < rng.choice(np.array([0.1, 0.4, 0.6]), (N, 8, 1))
    return pack(w, x, q, s, h, v, rng.choice(near, (N, 8, 16)))
def setup_inputs_ends(rng):
    def two(lo, hi, *sh): return np.where(rng.random(sh) < 0.5, lo, hi)
    x = np.where(rng.random((N, 8, 1, V)) < 0.5, two(0, 255, N, 8, 1, V), two(0, 255, N, 8, 16, V))
    s = np.where(rng.random((N, 8, 1, TY)) < 0.5, two(0, 255, N, 8, 1, TY), two(0, 255, N, 8, 16, TY))
    h = np.where(rng.random((N, 8, V)) < 0.9, two(0, TY - 1, N, 8, V), rng.integers(0, TY, (N, 8, V)))
    v = (rng.random((N, 8, V)) < 0.4).astype(np.int64)
    w = np.where(rng.random((N, 8, 16, V)) < 0.8, two(0, V - 1, N, 8, 16, V), rng.integers(0, V, (N, 8, 16, V)))
    q = np.where(rng.random((N, 8, 16, TY)) < 0.7, two(0, TY, N, 8, 16, TY), TY - 1)
    for c in (0, TY - 1): q[..., c] = np.where(rng.random((N, 8, 16)) < 0.85, two(0, TY - 1, N, 8, 16), TY)
    z = np.stack([rng.permutation(np.array([2, 3, 4, 5, 6, 8, 12, 16])) for r in range(N)]); z[:, 7] = 5
    t = np.where(np.argsort(rng.random((N, 8, 16)), axis=-1) < z[..., None], 0, 4080)
    c = cand(np.array([(255 * 1216) & (V - 1)]))[:, 0]
    v[:, 7, 0] = 1; v[:, 7, V - 1] = 0; v[:, 7, c[:2]] = 0; v[:, 7, c[2]] = 1; v[:, 7, c[15]] = 1
    x[:, 7] = np.where(v[:, 7] == 1, 0, 255)[:, None, :]
    lo = two(0, 255, N, 8, 1); lo[:, 7] = 0
    x[..., 0] = lo; x[..., V - 1] = 255 - lo; s[..., 0] = 255 - lo
    s[..., TY - 1] = np.where(rng.random((N, 8, 1)) < 0.5, lo, 255 - lo); s[:, 7, :, TY - 1] = 0
    h[..., 0] = TY - 1; h[..., V - 1] = 0
    q[0, :, 0] = TY; t[0] = 4080; t[0, :, 0] = 0
    return pack(w, x, q, s, h, v, t)
def setup_inputs_corners(rng):
    w0 = np.zeros((N, 8, 16, V), np.int64); x0 = w0.copy(); q0 = np.zeros((N, 8, 16, TY), np.int64); s0 = q0.copy(); h0 = np.zeros((N, 8, V), np.int64); v0 = h0.copy()
    all_ = V - 16
    plan_u = (all_, LN, LN + 1, LN - 1, 1, 0, all_, all_); plan_p = (SL, SL + 1, SL - 1, LN, 1, 0, 0, SL); plan_t = (RT, RT + 1, RT - 1, 0, 0, 0, LN, RT)
    for r in range(N):
        for g in range(8):
            live = rng.permutation(TY)[:32]; s = rng.integers(0, 256, (16, TY)); s[:, live[1::2]] = s[:, live[0::2]]
            q = np.where(rng.random((16, TY)) < 0.6, live[rng.integers(0, 32, (16, TY))], TY)
            q[np.array([0, 3, 7, 11])] = live[rng.integers(0, 32, (4, TY))]; q[15, live] = live
            z = 1 + rng.permutation(V - 2)[:16]; reg = np.setdiff1d(np.arange(V), z)
            k = rng.permutation(np.concatenate([np.arange(32), rng.integers(0, 32, V - 48)]))
            o = np.argsort(k, kind="stable"); n = np.bincount(k, minlength=32); b = np.add.accumulate(n) - n
            back = np.zeros(TY + 1, np.int64); back[live] = np.arange(32)
            pairs = np.arange(16)
            h = np.zeros(V, np.int64); h[reg] = live[k]; h[z] = live[(2 * pairs + 2) % 32]
            x = np.zeros((16, V), np.int64); x[:, reg] = np.clip(s[:, live[k]] + rng.integers(-3, 4, (16, V - 16)), 0, 255); x[:, z] = s[:, live[2 * pairs]]
            w = rng.integers(0, V, (16, V)); need = q[:, h[reg]]; kk = back[need]
            wr = np.where(need == TY, w[:, reg], reg[o[b[kk] + (n[kk] * rng.random(kk.shape)).astype(np.int64)]])
            wr[15] = np.where(rng.random(V - 16) < 0.5, reg, wr[15])
            for e in (0, V - 17): wr = np.where((need < TY) & (kk == k[e]) & (rng.random(kk.shape) < 0.3), reg[e], wr)
            w[:, reg] = wr
            if r == 0: nu, n1, n2 = plan_u[g], plan_p[g], plan_t[g]
            else:
                nu = int(rng.choice(np.array([0, 1, LN - 1, LN, LN, LN + 1, all_, all_])))
                n1 = int(rng.choice(np.array([0, 1, SL - 1, SL, SL + 1, LN - RT - 1]))); n2 = int(rng.choice(np.array([0, 1, RT - 1, RT, RT + 1, LN])))
            on = np.sort(rng.permutation(reg)[:nu]); v = np.ones(V, np.int64); v[on] = 0
            la = rng.permutation(on[:LN]); m = len(la); n1 = min(n1, m); n2 = min(n2, m - n1); n3 = min(m - n1 - n2, int(rng.integers(0, 40)))
            nd = np.zeros(m, np.int64); nd[:n1] = rng.integers(1, 4, n1); nd[n1 + n2:n1 + n2 + n3] = rng.integers(4, 6, n3)
            need = q[:, h[la]]; kk = back[need]
            at = np.argsort(np.argsort(np.where(need < TY, rng.random(need.shape), 2.0), axis=0), axis=0)
            kb = 2 * ((kk // 2 + 1 + rng.integers(0, 15, kk.shape)) % 16) + rng.integers(0, 2, kk.shape)
            new = np.where(at < nd, reg[o[b[kb] + (n[kb] * rng.random(kb.shape)).astype(np.int64)]], w[:, la])
            re_ = (np.arange(m) >= n1) & (np.arange(m) < n1 + n2)
            w[:, la] = np.where((at == 0) & re_, z[kk // 2], new)
            w0[r, g], x0[r, g], q0[r, g], s0[r, g], h0[r, g], v0[r, g] = w, x, q, s, h, v
    return pack(w0, x0, q0, s0, h0, v0, rng.choice(np.array([0, 1, 30, 60]), (N, 8, 16)))
def setup_inputs_full(rng):
    w = rng.integers(0, V, (N, 8, 16, V)); x = np.zeros((N, 8, 16, V), np.int64); q = np.full((N, 8, 16, TY), TY); s = rng.integers(0, 256, (N, 8, 16, TY))
    h = np.zeros((N, 8, V), np.int64); v = h.copy(); M = TY - 24; i = np.arange(V); edge = max(ST, LN) + LN; first = int(rng.integers(0, N))
    for a in range(N):
        r = (first + a) % N; role = a % 4; lo, hi = ((200, 241), (10, 41), (40, 121), (40, 121))[role]
        for g in range(8):
            ty = rng.permutation(TY); rest = ty[24:]
            b = rng.integers(lo, hi, (16, 1)); x[r, g] = b + rng.integers(-2, 3, (16, V))
            far = rng.integers(0, 21, (16, 8)); s[r, g][:, ty[:8]] = far if role == 0 else 255 - far
            s[r, g][:, ty[8:16]] = b + (2 * rng.integers(0, 2, (16, 8)) - 1) * rng.integers(5, 8, (16, 8)); s[r, g][:, ty[16:24]] = b
            sort = np.arange(M) % 4; at = np.argsort(rng.random((16, M)), axis=0)
            cnt = np.where(sort == 1, rng.integers(1, 4, M), np.where(sort == 2, rng.integers(1, 9, M), np.where(sort == 3, 1, 0)))
            pick = np.where(sort == 3, np.arange(M) // 4 % 8, rng.integers(0, 8, (16, M)))
            q[r, g][:, rest] = np.where(at < cnt, ty[8 * np.maximum(sort - 1, 0) + pick], TY)
            c = rng.integers(0, 4, V)
            if role == 0:
                c[:LN] = 1; v[r, g, LN:] = rng.random(V - LN) < 0.5
                if g % 4 == 3: c[:256] = 0
            elif role == 1: v[r, g] = rng.random(V) < 0.85
            elif role == 2: c = np.where(i < LN, 0, 2)
            else: c = np.where(i < edge, 1, 2); c[rng.permutation(LN)[:int(rng.integers(20, 29))]] = 0
            y = 4 * rng.integers(0, M // 4, V) + c
            if role == 2:
                o = np.arange(256, LN - 1, 4); goal = LN + rng.permutation(V - LN)[:len(o)]
                for k in (0, 1):
                    y[o + k] = 4 * (2 * rng.integers(0, M // 8, len(o)) + k) + 3
                    w[r, g, np.argmin(at[:, y[o + k]], axis=0), o + k] = goal
            h[r, g] = rest[y]
    for a in range(0, N - 1, 4):
        r, e = (first + a) % N, (first + a + 1) % N
        for g in (3, 7):
            k = np.arange(255 + SL, 255, -1); c = cand(np.add.reduce(WT[:, None] * x[r, g][:, k], axis=0) & (V - 1))
            top = np.max(x[e, g], axis=1) + 1; used = np.zeros(V, bool)
            for b in range(SL):
                if np.any(used[c[:, b]]): continue
                used[c[:, b]] = True; v[e, g, c[0, b]] = 1; v[e, g, c[15, b]] = 1
                x[e, g][:, c[0, b]] = top - (np.arange(16) == rng.integers(0, 16)); x[e, g][:, c[15, b]] = top
    return pack(w, x, q, s, h, v, 32 + rng.integers(0, 9, (N, 8, 16)))
def check_inputs(d):
    bad = []
    for k, lo, hi in (("wd", 0, V - 1), ("xs", 0, 255), ("rq", 0, TY), ("sg", 0, 255), ("hy", 0, TY - 1), ("vf", 0, 1), ("th", 0, 4080)):
        a = np.asarray(d[k]).astype(np.float64)
        if not (np.min(a) >= lo and np.max(a) <= hi): bad.append("range of " + k)
        elif np.any(a != np.floor(a)): bad.append("whole numbers of " + k)
    return bad
def reference(wd, xs, rq, sg, hy, vf, th):
    m = wd.astype(np.int64).reshape(N, 8, 16, V); x = xs.astype(np.float32).astype(np.int64).reshape(N, 8, 16, V)
    q = rq.astype(np.int64).reshape(N, 8, 16, TY); s = sg.astype(np.float32).astype(np.int64).reshape(N, 8, 16, TY)
    h = hy.astype(np.int64).reshape(N, 8, V); v = vf.reshape(N, 8, V) == 1; lim = th.astype(np.int64).reshape(N, 8, 16, 1)
    last = np.zeros(N, np.int64)
    for t in range(RO):
        d = 1 + t % (N - 1); order = (ST * t + np.arange(V)) % V
        m1, h1, v1 = m.copy(), h.copy(), v.copy(); now = np.zeros(N, np.int64)
        for r in range(N):
            e = (r + d) % N
            for g in range(8):
                a = order[~v[r, g][order]][:LN]
                w = m[r, g][:, a]; need = q[r, g][:, h[r, g][a]]
                other = (need < TY) & (h[r, g][w] != need)
                far = np.add.reduce(np.abs(x[r, g][:, w] - s[r, g][:, np.minimum(need, TY - 1)]), axis=0)
                fail = other & (far > lim[r, g] + (last[r] & 255))
                n = np.add.reduce(fail.astype(np.int64), axis=0); good = n == 0; much = n > 3
                now[r] += np.count_nonzero(good)
                v1[r, g, a[good]] = True
                y = h[r, g][a[much]]; h1[r, g, a[much]] = ((y * y >> 4) + 5 * y + n[much]) & (TY - 1)
                i = np.flatnonzero((n > 0) & (n < 4))[:SL]
                if len(i) > 0:
                    z = x[r, g][:, a[i]]; u = np.add.reduce(WT[:, None] * z, axis=0) & (V - 1); c = cand(u); k = np.arange(len(i))
                    gap = np.add.reduce(np.abs(x[e, g][:, c] - z[:, None, :]), axis=0)
                    gap = np.where(v[e, g][c], gap, 4096); b = np.argmin(gap, axis=0)
                    take = fail[:, i] & (gap[b, k] < 4096)
                    m1[r, g][:, a[i]] = np.where(take, m[e, g][:, c[b, k]], w[:, i])
                j = np.flatnonzero(good & np.any(other, axis=0))[:RT]
                if len(j) > 0:
                    p = np.argmax(other[:, j], axis=0); name, one = np.unique(w[p, j], return_index=True)
                    h1[r, g, name] = need[p, j][one]; v1[r, g, name] = False
        m, h, v, last = m1, h1, v1, now
    return {"ym": m.reshape(N, 128, V).astype(np.float32), "yh": h.astype(np.float32), "yv": v.astype(np.float32)}

@@ -1,0 +1,743 @@
+from concourse.bass import DstId, RemoteDMATransfer
+from concourse.mybir import dt, AluOpType, AxisListType, ActivationFunctionType
+
+N = 6
+V, TY, LN, SL, RT, RO, ST = 1024, 2048, 384, 48, 16, 4, 320
+CH = [112, 112, 96, 64]
+HV = [0]
+SPLIT = [(0, 64)]
+NC = LN // 16
+BW = 144
+NB = V // 16
+
+BUFS = {
+    "WD": (V, "int32"), "XS": (V, "bfloat16"), "RQ": (TY, "int32"), "SS": (TY + 16, "bfloat16"), "THI": (1, "int32"),
+    "HYB": (64, "int32"), "VFB": (64, "int32"), "HT": (V + 32, "bfloat16"), "PERM": (V, "bfloat16"),
+    "PERMK": (LN, "bfloat16"), "PLD": (LN, "bfloat16"), "P2": (LN, "bfloat16"), "NEWP": (LN, "bfloat16"),
+    "K16": (LN, "uint16"), "W16": (LN, "uint16"), "KF": (LN, "float16"), "WF": (LN, "float16"),
+    "DAT": (LN, "bfloat16"), "OTB": (LN, "bfloat16"), "FB": (LN, "bfloat16"), "QP": (LN, "float32"),
+    "SGA": (16 * LN, "bfloat16"), "HGA": (16 * LN, "bfloat16"), "MXA": (16 * LN, "bfloat16"),
+    "CX": (LN, "int32"), "C15": (LN, "int32"), "CT1": (LN, "int32"), "CT2": (LN, "int32"), "CG": (128, "int32"), "PII": (16, "int32"),
+    "PF": (16, "float32"), "OH": (16, "float32"), "WC": (16, "float32"),
+    "GSEL": (128, "bfloat16"), "GSELN": (128, "bfloat16"), "GSELH": (128, "float16"),
+    "BASE": (BW, "bfloat16"), "BASEH": (BW, "float16"), "BH0": (BW, "float16"), "WR": (16 * BW, "bfloat16"),
+    "BE": (BW, "bfloat16"), "BA": (BW, "bfloat16"), "BSX": (BW, "bfloat16"), "BJ": (BW, "bfloat16"), "BV": (BW, "bfloat16"),
+    "BVN": (BW, "bfloat16"), "B2": (BW, "bfloat16"), "BM1": (BW, "bfloat16"), "B16": (BW, "bfloat16"), "BHF": (BW, "bfloat16"), "NID": (128, "bfloat16"), "IKP": (128, "bfloat16"),
+    "HTS": (V + 32, "bfloat16"), "GAB": (768, "bfloat16"), "BU": (BW, "bfloat16"),
+    "GA": (128, "bfloat16"), "GUU": (128, "bfloat16"), "GAA": (128, "bfloat16"), "GCT": (128, "bfloat16"),
+    "G16": (128, "bfloat16"), "GHE": (128, "bfloat16"),
+    "TGE": (128, "bfloat16"), "TST": (128, "bfloat16"), "TSN": (128, "bfloat16"), "PL0": (128, "float16"), "PL1": (128, "float16"),
+    "ID": (128, "bfloat16"), "IH": (128, "float16"), "NIH": (128, "float16"), "IKH": (128, "float16"),
+    "I8": (128, "bfloat16"), "NI8": (128, "bfloat16"), "I22": (128, "bfloat16"), "NI22": (128, "bfloat16"),
+    "ON": (128, "bfloat16"), "ONN": (128, "bfloat16"), "IA": (V, "bfloat16"), "IB": (V, "bfloat16"),
+    "D2": (128, "bfloat16"), "D3": (128, "bfloat16"), "D7": (128, "bfloat16"), "D8": (128, "bfloat16"), "MC": (LN, "bfloat16"), "RST": (LN, "float32"),
+    "QC": (72, "float16"), "QT": (72, "bfloat16"), "SC": (2, "bfloat16"), "NT": (256, "bfloat16"), "JV": (256, "float16"), "JC": (256, "float16"),
+    "RR": (256, "int32"), "RC": (8, "int32"), "RCF": (8, "float32"), "UPM": (16, "float16"), "JNK": (1, "float32"),
+    "PC": (704, "int32"), "PCB": (704, "bfloat16"), "TI": (512, "int32"), "THF": (1, "float32"),
+    "V16": (64, "bfloat16"), "VJ": (64, "float16"), "CT16": (128, "bfloat16"), "OFF": (64, "uint16"),
+    "Y16": (NC, "uint16"), "A16": (NC, "uint16"), "YI": (NC, "int32"), "HB": (4 * NC, "int32"),
+    "CC": (4 * NC, "bfloat16"), "PRO": (72, "bfloat16"), "OX": (NC, "bfloat16"), "CP": (128, "bfloat16"), "MU": (72, "float16"), "OF2": (NC, "uint16"),
+    "PT": (2, "float32"), "HL": (6 * NC, "int32"), "HLV": (72, "bfloat16"),
+    "LJ": (NC, "uint16"), "JP": (2, "uint16"), "GI": (16, "int32"), "OT": (16, "bfloat16"), "FST": (16, "bfloat16"),
+    "WKL": (48, "int32"), "PRD": (48, "float16"), "TWC": (1, "float32"), "EQ": (17, "float32"), "BAD": (1, "float32"), "TG": (2, "uint16"),
+    "OKT": (16, "bfloat16"), "NK": (16, "bfloat16"), "BS": (1, "float32"), "BI": (2, "int32"), "TB": (1, "float32"),
+    "RX": (48 * 6, "int32"), "RU": (96, "float32"), "RB": (48 * 3, "bfloat16"), "RF": (48 * 3, "float32"), "RH": (48, "float16"),
+    "RL": (104, "uint16"), "XA": (768, "bfloat16"), "HEG": (768, "bfloat16"), "MX": (768, "bfloat16"), "KS": (768, "float32"), "WN": (48, "int32"),
+    "YM": (V, "float32"), "Y8": (2 * V, "float32"),
+}
+PARTS = {"QT": 48, "SC": 48, "NT": 64, "CT16": 64, "CP": 48, "Y8": 8}
+PACKED = ["CG", "GSEL", "GSELN", "GSELH", "BASE", "BASEH", "BH0", "WR", "BE", "BA", "BSX", "BJ", "BV", "BVN", "B2", "BM1", "B16", "BHF", "NID", "IKP", "BU",
+          "GA", "GUU", "GAA", "GCT", "G16", "GHE", "TGE", "TST", "TSN", "PL0", "PL1", "ID", "IH", "NIH", "IKH", "I8", "NI8",
+          "I22", "NI22", "ON", "ONN", "D2", "D3", "D7", "D8", "MC", "QC", "QT", "SC", "NT", "JV", "JC", "RR", "RC", "UPM", "JNK", "PF", "OH", "WC"]
+PLACE = {}
+SCRATCH = {}
+for _n in BUFS:
+    _c, _d = BUFS[_n]
+    if _n in PACKED:
+        _k = "k" + _d
+        _o = SCRATCH[_k][1][1] if _k in SCRATCH else 0
+        PLACE[_n] = (_k, _o)
+        SCRATCH[_k] = ("sbuf", [128, _o + (_c + 15) // 16 * 16], _d)
+    else:
+        PLACE[_n] = (_n, 0)
+        SCRATCH[_n] = ("sbuf", [PARTS.get(_n, 128), _c], _d)
+SCRATCH["XE"] = ("sbuf", [128, RO * V], "bfloat16")
+SCRATCH["HE"] = ("sbuf", [128, RO * V], "bfloat16")
+SCRATCH["WE"] = ("sbuf", [128, RO * V], "int32")
+for _i in range(8):
+    SCRATCH["b%d" % _i] = ("psum", [128, 512], "float32")
+
+LOADS = ["WD", "XS", "RQ", "SS", "THI", "HYB", "VFB"]
+SEMAPHORES = ["sv", "ss", "st", "sg", "oym", "oyh", "oyv"] + ["ld" + n for n in LOADS]
+for _t in range(RO):
+    for _k in ("X", "H", "W"):
+        SEMAPHORES += ["arr%s%d" % (_k, _t), "loc%s%d" % (_k, _t)]
+
+A = AluOpType
+CYC = 0.83 * 1.25
+GET, PUT, WAKE = 1.6, 3.8, 0.1
+PEC = 0.417 * 1.25
+SEED, AMP = 0, 0.0
+
+
+def R(name, c0=0, c1=None, step=1, p=None):
+    if c1 is None:
+        c1 = BUFS[name][0] if name in BUFS else SCRATCH[name][1][1]
+    if p is None:
+        p = PARTS.get(name, 128)
+    name, o = PLACE.get(name, (name, 0))
+    return ("ap", name, c0 + o, c1 + o, step, p)
+
+
+def X(name, c0, c1, off, o0, o1):
+    return ("ind", name, c0, c1, off, o0, o1)
+
+
+def ap(T, r):
+    if r[0] == "ap":
+        _, n, c0, c1, step, p = r
+        if step == 1:
+            return T[n][0:p, c0:c1]
+        return T[n][0:p, c0:c1:step]
+    _, n, c0, c1, off, o0, o1 = r
+    return T[n][:, c0:c1].indirect(T[off][:, o0:o1])
+
+
+def width(r):
+    if r[0] == "ind":
+        return 16 * (r[6] - r[5])
+    return -(-(r[3] - r[2]) // r[4])
+
+
+def touched(r):
+    return [(r[1], r[2], r[3])]
+
+
+def lists(r):
+    return [(r[4], r[5], r[6])] if r[0] == "ind" else []
+
+
+def psum(r):
+    return r[0] == "ap" and SCRATCH[r[1]][0] == "psum"
+
+
+def two(r):
+    return SCRATCH[r[1]][2] in ("bfloat16", "float16", "uint16") and r[0] == "ap"
+
+
+def make_program():
+    ops = []
+
+    def add(q, call, reads, writes, cost, **kw):
+        rd, wr = [], []
+        for r in reads:
+            if isinstance(r, tuple):
+                rd += touched(r) + lists(r)
+        for r in writes:
+            wr += touched(r)
+            rd += lists(r)
+        o = {"q": q, "call": call, "rd": rd, "wr": wr, "cost": cost, "incs": 1, "lat": 0.0}
+        o.update(kw)
+        ops.append(o)
+        return o
+
+    def price(refs, out, mult, q):
+        n = max([width(r) for r in refs])
+        if out[0] == "ind":
+            return 0.05 + PUT * CYC / 1000 * width(out)
+        if any(r[0] == "ind" for r in refs):
+            return 0.06 + GET * CYC / 1000 * n
+        return max(64, n * mult) * CYC / 1000 + (0.01 if q == "v" else 0.06)
+
+    def tc(q, out, in_):
+        if q == "v":
+            f = lambda g, T: g.vector.tensor_copy(out=ap(T, out), in_=ap(T, in_))
+        else:
+            f = lambda g, T: g.scalar.activation(ap(T, out), ap(T, in_), ActivationFunctionType.Copy)
+        add(q, f, [in_], [out], price([in_, out], out, 0.5 if two(in_) and two(out) and q == "v" else 1, q))
+
+    def act(out, in_, func, bias=None):
+        def f(g, T):
+            if bias is None:
+                return g.scalar.activation(ap(T, out), ap(T, in_), func)
+            return g.scalar.activation(ap(T, out), ap(T, in_), func, bias=ap(T, bias))
+        add("s", f, [in_, bias], [out], price([in_], out, 1, "s"))
+
+    def by(out, in_, col):
+        add("s", lambda g, T: g.scalar.activation(ap(T, out), ap(T, in_), ActivationFunctionType.Copy,
+                                                  scale=ap(T, col) if isinstance(col, tuple) else col),
+            [in_, col], [out], price([in_], out, 1, "s"))
+
+    def tt(out, a, b, op):
+        add("v", lambda g, T: g.vector.tensor_tensor(out=ap(T, out), in0=ap(T, a), in1=ap(T, b), op=op), [a, b], [out],
+            price([a, b], out, 1 if psum(a) or psum(b) else 2, "v"))
+
+    def ts(out, a, s1, op0, s2=None, op1=None):
+        def f(g, T):
+            x1 = ap(T, s1) if isinstance(s1, tuple) else s1
+            x2 = ap(T, s2) if isinstance(s2, tuple) else s2
+            if op1 is None:
+                return g.vector.tensor_scalar(out=ap(T, out), in0=ap(T, a), scalar1=x1, scalar2=None, op0=op0)
+            return g.vector.tensor_scalar(out=ap(T, out), in0=ap(T, a), scalar1=x1, scalar2=x2, op0=op0, op1=op1)
+        add("v", f, [a, s1, s2], [out], price([a], out, 0.5 if two(a) and two(out) else 1, "v"))
+
+    def red(out, a, op):
+        add("v", lambda g, T: g.vector.tensor_reduce(out=ap(T, out), in_=ap(T, a), axis=AxisListType.X, op=op), [a], [out], price([a], out, 1, "v"))
+
+    def scan(out, d0, d1, init, op0, op1):
+        add("v", lambda g, T: g.vector.tensor_tensor_scan(out=ap(T, out), data0=ap(T, d0), data1=ap(T, d1), initial=init, op0=op0, op1=op1),
+            [d0, d1], [out], price([d0, d1], out, 1, "v"))
+
+    def fill(out, c):
+        add("v", lambda g, T: g.vector.memset(ap(T, out), c), [], [out], price([out], out, 1, "v"))
+
+    def mm(items):
+        last = len(items) - 1
+        sig = [i for i, x in enumerate(items) if x[4] or i == last]
+
+        def f(g, T, sem=None):
+            for i, (o, l, r, s, e) in enumerate(items):
+                c = g.tensor.matmul(out=ap(T, o), lhsT=ap(T, l), rhs=ap(T, r), start=s, stop=e)
+                if sem is not None and i in sig:
+                    c.then_inc(sem, 1)
+        rd, wr = [], []
+        for x in items:
+            rd += [x[1], x[2]]
+            wr += [x[0]]
+        add("t", f, list(dict.fromkeys(rd)), list(dict.fromkeys(wr)), sum(max(64, width(x[2])) for x in items) * PEC / 1000, incs=len(sig))
+
+    def chain(out, pairs, first=True, last=True):
+        k = len(pairs) - 1
+        mm([(out, l, r, first and i == 0, last and i == k) for i, (l, r) in enumerate(pairs)])
+
+    def sh(name, m):
+        return R(name, 15 - m, 15 - m + 128)
+
+    def wr(r, m):
+        return R("WR", r * BW + 15 - m, r * BW + 15 - m + 128)
+
+    def wrap(mat, src, c0, c1):
+        return [(sh(mat, r), R(src, c0 + r, c1, 16)) for r in range(16)]
+
+    def send(kind, t, src):
+        add("g", (kind, t, src), [src], [], 0.3, kind="send", sem="loc%s%d" % (kind, t), lat=6.0)
+
+    def recv(kind, t, dst):
+        add(None, None, [], [dst], 0.0, kind="recv", sem="arr%s%d" % (kind, t), lat=14.0 + 30 * t)
+
+    def load(q, dst, name, sem, lat):
+        def f(g, T):
+            return (g.sync if q == "y" else g.scalar).dma_start(out=ap(T, dst), in_=T[name][:, :])
+        add(q, f, [], [dst], 0.1, kind="dma", sem=sem, lat=lat)
+
+    def store(q, name, src, sem):
+        def f(g, T):
+            return (g.sync if q == "y" else g.scalar).dma_start(out=T[name][:, :], in_=ap(T, src))
+        add(q, f, [src], [], 0.1, kind="dma", sem=sem, lat=3.0)
+
+    load("y", R("HYB"), "hy", "ldHYB", 2.0)
+    load("s", R("XS"), "xs", "ldXS", 3.5)
+    load("y", R("VFB"), "vf", "ldVFB", 2.0)
+    load("y", R("WD"), "wd", "ldWD", 6.0)
+    load("s", R("RQ"), "rq", "ldRQ", 9.0)
+    load("y", R("SS", 0, TY), "sg", "ldSS", 9.0)
+    load("y", R("THI"), "th", "ldTHI", 3.0)
+
+    add("g", lambda g, T: g.iota(T["CX"][:, :], [[1, LN]], 0, 0), [], [R("CX")], 0.13 + 2 * LN * CYC / 1000)
+    add("g", lambda g, T: g.iota(T["PII"][:, 0:1], [[1, 1]], 0, 1), [], [R("PII", 0, 1)], 0.14)
+    for n, pat in (("IA", [[1, 256], [0, 4]]), ("IB", [[0, 256], [1, 4]])):
+        add("g", lambda g, T, n=n, pat=pat: g.iota(T[n][:, :], pat, 0, 0, allow_small_or_imprecise_dtypes=True),
+            [], [R(n)], 0.13 + 2 * V * CYC / 1000)
+    c1 = lambda n, j: R(n, j, j + 1)
+    P_, PM, PG, P15, K24, PM24, P64 = [c1("PF", j) for j in range(7)]
+    ts(c1("PII", 1), c1("PII", 0), 15, A.bitwise_and)
+    ts(c1("PII", 2), c1("PII", 0), 4, A.arith_shift_right)
+    tc("v", R("PF", 0, 3), R("PII", 0, 3))
+    ts(P15, PG, 16.0, A.mult, 15.0, A.add)
+    ts(K24, P_, 24.0, A.is_ge)
+    ts(PM24, P_, -24.0, A.add)
+    ts(P64, PM, 64.0, A.mult)
+    ts(R("C15"), R("CX"), 15, A.bitwise_and)
+    ts(R("CG"), R("CX", 0, 128), 4, A.arith_shift_right)
+    ts(R("OH"), R("C15", 0, 16), PM, A.is_equal)
+    ts(R("BASE"), R("CX", 0, BW), P15, A.is_equal)
+    ts(R("GSEL"), R("CG"), PG, A.is_equal)
+    oh = lambda j: c1("OH", j)
+    for r in range(16):
+        by(R("WR", r * BW, (r + 1) * BW), R("BASE"), oh(r))
+    ts(c1("WC", 9), PM, 10.0, A.mult, 1.0, A.add)
+    ts(R("BU"), R("BASE"), c1("WC", 9), A.mult)
+
+    ts(c1("WC", 8), PM, 1.0, A.is_gt, oh(6), A.subtract)
+    ts(R("ID"), R("CX", 0, 128), P_, A.is_equal)
+    for k in (2, 3, 7, 8):
+        by(R("D%d" % k), R("ID"), oh(k))
+
+    sx, uu = R("b0", 0, 64), R("b1", 0, 64)
+    chain(sx, [(sh("BASE", b), R("XS", 64 * b, 64 * b + 64)) for b in range(16)])
+    chain(uu, [(sh("BU", b), R("XS", 64 * b, 64 * b + 64)) for b in range(16)])
+    pc = lambda j: R("PC", 64 * j, 64 * j + 64)
+    ti = lambda j: R("TI", 64 * j, 64 * j + 64)
+    kinds = [0, 1, 6, 4, 5, 9, 10, 11, 12]
+
+    def split(j, src, s, m):
+        ts(pc(j), src, s, A.arith_shift_right)
+        ts(pc(j + 1), src, m, A.bitwise_and)
+    split(0, R("HYB"), 3, 7)
+    tc("v", pc(2), R("VFB"))
+    tc("v", R("PCB", 0, 192), R("PC", 0, 192))
+    for h in range(2):
+        mm([(R("b%d" % (4 + h), 64 * b, 64 * b + 64), wr(8 * h + b, 6), R("PCB", 128, 192), True, True) for b in range(8)])
+        tc("s", R("SGA", 512 * h, 512 * h + 512), R("b%d" % (4 + h)))
+    tc("v", ti(1), sx)
+    split(3, ti(1), 4, 15)
+    tc("v", ti(2), uu)
+    ts(ti(3), ti(2), 1023, A.bitwise_and)
+    ts(ti(4), ti(3), 2.0, A.mult, 1.0, A.add)
+    split(5, ti(4), 3, 7)
+    tt(ti(5), ti(3), ti(3), A.mult)
+    ts(ti(6), ti(5), 5, A.arith_shift_right)
+    tt(ti(7), ti(6), ti(3), A.add)
+    ts(ti(0), ti(7), 1023, A.bitwise_and)
+    split(7, ti(0), 2, 3)
+    tc("v", R("PCB", 192, 576), R("PC", 192, 576))
+    fill(R("HT", V, V + 32), 0.0)
+    for h in range(2):
+        o = R("b%d" % (2 + h))
+        mm([(o, R("D2"), R("IA", 512 * h, 512 * h + 512), True, False)])
+        for sub in (kinds[:3], kinds[3:]):
+            mm([(R("b%d" % (2 + h), 64 * b, 64 * b + 64), wr(8 * h + b, k), R("PCB", 64 * kinds.index(k), 64 * kinds.index(k) + 64), False, False)
+                for b in range(8) for k in sub])
+        mm([(o, R("D3"), R("IB", 512 * h, 512 * h + 512), False, True)])
+        tc("v" if h else "s", R("HT", 512 * h, 512 * h + 512), R("b%d" % (2 + h)))
+    by(R("HTS"), R("HT"), c1("WC", 8))
+
+    def wcol(j, a, x, b, y):
+        if y == 1:
+            ts(c1("WC", j), oh(a), float(x), A.mult, oh(b), A.add)
+        else:
+            ts(c1("WC", 10 + j % 2), oh(b), float(y), A.mult)
+            ts(c1("WC", j), oh(a), float(x), A.mult, c1("WC", 10 + j % 2), A.add)
+    wcol(0, 0, 8, 1, 1)
+    wcol(1, 2, 4, 3, 1)
+    wcol(2, 4, -16, 5, -1)
+    wcol(3, 7, 4, 8, 1)
+    wcol(4, 9, 8, 10, 1)
+    wcol(5, 11, 4, 12, 1)
+    ts(c1("WC", 6), oh(6), -131072.0, A.mult)
+    ts(c1("WC", 7), oh(6), -1024.0, A.mult)
+    for n, s in (("BV", oh(6)), ("BE", c1("WC", 0)), ("BA", c1("WC", 1)), ("BSX", c1("WC", 2)), ("BJ", c1("WC", 3)),
+                 ("BVN", c1("WC", 7)), ("B2", 2.0), ("BM1", -1.0), ("B16", 16.0), ("BHF", 0.5)):
+        by(R(n), R("BASE"), s)
+    ts(R("CT1", 0, 128), R("C15", 0, 128), PM, A.is_le)
+    tt(R("TGE"), R("CT1", 0, 128), R("GSEL"), A.mult)
+    ts(R("CT2", 0, 128), R("C15", 0, 128), PM, A.is_gt)
+    tt(R("TST"), R("CT2", 0, 128), R("GSEL"), A.mult)
+    ts(R("TSN"), R("TST"), -1.0, A.mult)
+    for n, s in (("IH", 1.0), ("NIH", -1.0), ("IKH", 1024.0)):
+        ts(R(n), R("ID"), s, A.mult)
+    for n, s in (("NID", -1.0), ("I8", 8192.0), ("NI8", -8192.0), ("I22", 4194304.0), ("NI22", -4194304.0), ("IKP", c1("WC", 8))):
+        by(R(n), R("ID"), s)
+    for t in range(RO):
+        k = 64 * t
+        ts(R("RR", k, k + 64), R("CX", 0, 64), float((64 - ST // 16 * t) % 64), A.add)
+        ts(R("CT1", k, k + 64), R("RR", k, k + 64), 63, A.bitwise_and)
+        ts(c1("RC", t), c1("PII", 0), float((64 - ST // 16 * t) % 64), A.add)
+        ts(c1("RC", 4 + t), c1("RC", t), 63, A.bitwise_and)
+        tc("v", c1("RCF", t), c1("RC", 4 + t))
+        ts(R("NT", k, k + 64, p=64), R("CT1", k, k + 64, p=64), R("RCF", t, t + 1, p=64), A.is_ge, -1.0, A.mult)
+        ts(R("JV", k, k + 64), R("CT1", k, k + 64), 16.0, A.mult, PM, A.add)
+        ts(R("JC", k, k + 64), R("JV", k, k + 64), -1.0, A.mult, 1023.0, A.add)
+    ts(R("GSELN"), R("GSEL"), -1.0, A.mult)
+    tc("v", R("GSELH"), R("GSEL"))
+    tc("v", R("BASEH"), R("BASE"))
+    ts(R("BH0"), R("BASE"), oh(0), A.mult)
+    for n, s in (("GA", c1("WC", 1)), ("GUU", c1("WC", 4)), ("GAA", c1("WC", 5)), ("GHE", c1("WC", 6)), ("G16", 16.0)):
+        by(R(n), R("GSEL"), s)
+    tt(R("NEWP", 0, 128), R("GUU"), R("C15", 0, 128), A.mult)
+    tt(R("GCT"), R("NEWP", 0, 128), R("GAA"), A.add)
+    for j, n in ((0, "PL0"), (1, "PL1")):
+        ts(R("CT1", 128 * j, 128 * j + 128), R("C15", 0, 128), float(j), A.is_equal)
+        tt(R(n), R("CT1", 128 * j, 128 * j + 128), R("GSEL"), A.mult)
+    fill(R("ON"), 1.0)
+    fill(R("ONN"), -1.0)
+    tc("v", R("MC"), R("C15"))
+    ts(R("RST"), R("C15"), 0.0, A.is_equal, 1000000.0, A.mult)
+    ts(R("QC", 0, 24), R("CX", 0, 24), 0.0, A.mult, 383.0, A.add)
+    ts(R("QC", 24, 48), R("CX", 0, 24), 0.0, A.mult)
+    ts(R("QC", 48, 72), R("CX", 0, 24), 16.0, A.mult, PM, A.add)
+    q48 = lambda n, a, b: R(n, a, b, p=48)
+    ts(q48("QT", 0, 24), q48("CX", 0, 24), q48("PF", 0, 1), A.is_gt, -1.0, A.mult)
+    ts(q48("QT", 24, 48), q48("CX", 0, 24), q48("PF", 5, 6), A.is_gt, q48("PF", 4, 5), A.mult)
+    tt(q48("RU", 0, 24), q48("QT", 0, 24), q48("QT", 24, 48), A.subtract)
+    ts(q48("QT", 48, 72), q48("RU", 0, 24), q48("PF", 4, 5), A.add)
+    ts(q48("SC", 0, 1), q48("PF", 4, 5), -1.0, A.mult, 1.0, A.add)
+    tc("v", q48("SC", 1, 2), q48("PF", 4, 5))
+    ts(R("UPM"), R("CX", 0, 16), PM, A.is_le, 4096.0, A.mult)
+    ts(R("JNK"), PM, 1032.0, A.add)
+    fill(R("SS", TY, TY + 16), 0.0)
+    ts(R("THF"), R("THI"), -1.0, A.mult, -8192.5, A.add)
+    tc("v", R("TB"), R("THF"))
+
+    send("H", 0, R("HT", 0, V))
+    send("X", 0, R("XS"))
+    send("W", 0, R("WD"))
+    for t in range(1, RO):
+        send("X", t, R("XS"))
+    for t in range(RO):
+        for k, n in (("X", "XE"), ("H", "HE"), ("W", "WE")):
+            recv(k, t, R(n, V * t, V * t + V))
+
+    cc = lambda j, m=1: R("CC", NC * j, NC * (j + m))
+    for t in range(RO):
+        if t:
+            send("H", t, R("HT", 0, V))
+            send("W", t, R("WD"))
+        kt = 64 * t
+        chain(R("b5", 0, 64), wrap("BV", "HT" if t else "SGA", 0, V))
+        tc("v", R("V16"), R("b5", 0, 64))
+        tt(R("VJ"), R("b5", 0, 64), R("JC", kt, kt + 64), A.mult)
+        chain(R("b6", 0, 128, p=64), [(R("V16"), R("GSEL"))])
+        tc("v", R("CT16"), R("b6", 0, 128, p=64))
+        chain(R("b5", 0, 64), [(R("IH"), R("JV", kt, kt + 64)), (R("TGE"), R("V16")), (R("IH"), R("VJ")), (R("CT16"), R("NT", kt, kt + 64))])
+        tc("v", R("OFF"), R("b5", 0, 64))
+        for a, b in SPLIT:
+            tc("v", X("PERM", 0, V, "OFF", a, b), R("HT", 16 * a, 16 * b))
+        chain(R("b6", 0, NC), wrap("BE", "PERM", 0, LN))
+        tc("v", R("Y16"), R("b6", 0, NC))
+        chain(R("b5", 0, NC), wrap("BA", "PERM", 0, LN))
+        tc("v", R("A16"), R("b5", 0, NC))
+        for a, b in ((0, 8), (8, NC)):
+            tc("v", R("K16", 16 * a, 16 * b), X("RQ", 0, TY, "Y16", a, b))
+        for a, b in ((0, 8), (8, NC)):
+            tc("v", R("W16", 16 * a, 16 * b), X("WD", 0, V, "A16", a, b))
+        tc("v", R("KF"), R("K16"))
+        tc("v", R("WF"), R("W16"))
+        ts(R("DAT"), R("K16"), 2048.0, A.is_ge)
+        chain(R("b4", 0, LN), [(R("ID"), R("PERM", 0, LN)), (R("D7"), R("IA", 0, LN)), (R("D8"), R("IB", 0, LN))])
+        tc("s", R("PLD"), R("b4", 0, LN))
+        z, nn = R("b7", 0, NC), R("b7", NC, 2 * NC)
+        chain(z, wrap("BVN", "PERM", 0, LN) + wrap("BM1", "DAT", 0, LN), last=False)
+        tc("v", R("YI"), R("Y16"))
+        hb = lambda j: R("HB", NC * j, NC * j + NC)
+        tt(hb(0), R("YI"), R("YI"), A.mult)
+        ts(hb(1), hb(0), 4, A.arith_shift_right)
+        ts(hb(2), R("YI"), 5.0, A.mult, 8.0, A.add)
+        tt(hb(3), hb(1), hb(2), A.add)
+        l0 = 0
+        for i, L in enumerate(CH):
+            l1 = l0 + L
+            g0, g1 = 16 * l0, 16 * l1
+            E, D = R("b%d" % (i % 2), 0, L), R(("b2", "b3", "b5", "b6")[i % 4], 0, L)
+            sl = lambda n: R(n, l0, l1)
+            tc("s", R("SGA", g0, g1), X("SS", 0, TY + 16, "K16", l0, l1))
+            tc("v" if i in HV else "s", R("HGA", g0, g1), X("HT", 0, V, "W16", l0, l1))
+            tt(R("MXA", g0, g1), X("XS", 0, V, "W16", l0, l1), R("SGA", g0, g1), A.max)
+            pick = lambda m, n: [(sh(m, p), R(n, g0 + p, g1, 16)) for p in range(16)]
+            chain(E, pick("BE", "HGA") + [(R("NIH"), sl("KF"))])
+            ts(sl("OTB"), E, 0.0, A.not_equal)
+            chain(D, [(R("NI8"), sl("DAT"))] + pick("BM1", "SGA"), last=False)
+            chain(D, pick("BSX", "HGA"), first=False, last=False)
+            chain(D, pick("B2", "MXA"), first=False, last=False)
+            chain(D, [(R("I8"), sl("OTB"))], first=False)
+            act(sl("FB"), D, ActivationFunctionType.Sign, R("TB"))
+            chain(R("b4", 0, L), [(R("IH"), sl("WF")), (R("IKH"), sl("KF")), (R("NI22"), sl("DAT")), (R("I22"), sl("OTB"))])
+            tc("s", sl("QP"), R("b4", 0, L))
+            l0 = l1
+        chain(z, wrap("BASE", "OTB", 0, LN), first=False, last=False)
+        chain(z, wrap("B16", "FB", 0, LN), first=False)
+        chain(nn, wrap("BHF", "FB", 0, LN))
+        for j, b in ((1, 1.0), (2, 32.0), (3, 128.0)):
+            ts(cc(j), z, b - 256.0, A.is_ge)
+        ts(R("OX"), z, -255.0, A.is_lt)
+        tt(R("PRO", 0, 48), cc(1, 2), cc(2, 2), A.subtract)
+        tt(R("PRO", 48, 72), R("OX"), cc(3), A.add)
+        hl = lambda j: R("HL", NC * j, NC * j + NC)
+        ts(R("HLV", 48, 72), z, -224.0, A.is_lt)
+        tt(hl(2), nn, hb(3), A.add)
+        chain(R("b5", 0, 128, p=48), [(cc(1, 2), R("GSEL")), (cc(2, 2), R("GSELN"))])
+        tc("v", R("CP"), R("b5", 0, 128, p=48))
+        mm([(R("b6", 0, 72), R("IH"), R("QC"), True, False), (R("b6", 0, 24), R("TSN"), R("PRO", 0, 24), False, False),
+            (R("b6", 24, 48), R("TST"), R("PRO", 24, 48), False, False), (R("b6", 48, 72), R("TSN"), R("PRO", 0, 24), False, False),
+            (R("b6", 48, 72), R("TSN"), R("PRO", 24, 48), False, False), (R("b6", 0, 72), R("CP"), R("QT"), False, True)])
+        tt(R("MU"), R("b6", 0, 72), R("PRO"), A.mult)
+        chain(R("b5", 0, NC), [(R("IH"), R("MU", 24 * j, 24 * j + 24)) for j in range(3)])
+        tc("v", R("OF2"), R("b5", 0, NC))
+        chain(R("b6", 0, 2), [(R("CP"), R("SC"))])
+        tc("v", R("PT"), R("b6", 0, 2))
+        tc("v", X("P2", 0, LN, "OF2", 0, NC), R("PLD"))
+        ts(hl(3), hl(2), 2047, A.bitwise_and)
+        tt(hl(4), hl(3), R("YI"), A.subtract)
+        tt(hl(5), hl(4), cc(3), A.mult)
+        tt(hl(2), hl(5), R("YI"), A.add)
+        ts(hl(0), hl(2), 3, A.arith_shift_right)
+        ts(hl(1), hl(2), 7, A.bitwise_and)
+        tc("v", R("HLV", 0, 48), R("HL", 0, 48))
+        mm([x for r in range(16) for x in [(R("b4", r, LN, 16), R("IKP"), R("PERM", r, LN, 16), True, False)] +
+            [(R("b4", r, LN, 16), wr(r, k), R("HLV", 24 * i, 24 * i + 24), False, i == 2) for i, k in enumerate((0, 1, 6))]])
+        tc("s", R("PERM", 0, LN), R("b4", 0, LN))
+        tc("s", R("HT", 0, V), X("PERM", 0, V, "OFF", 0, 64))
+        chain(R("b6", 0, NC), wrap("BJ", "P2", 0, LN))
+        tc("v", R("JP", 0, 1), R("b6", NC - 1, NC))
+        tc("v", R("LJ"), R("b6", 0, NC))
+        ts(R("OT"), X("QP", 0, LN, "JP", 0, 1), 4194304.0, A.is_ge)
+        tc("v", R("GI"), X("QP", 0, LN, "JP", 0, 1))
+        chain(R("b5", 0, 16), [(R("TST"), R("OT"))])
+        ts(R("WKL", 0, 16), R("GI"), 1023, A.bitwise_and)
+        ts(R("WKL", 16, 32), R("GI"), 13, A.arith_shift_right, 255, A.bitwise_and)
+        ts(R("WKL", 32, 48), R("GI"), 10, A.arith_shift_right, 7, A.bitwise_and)
+        tt(R("FST"), R("OT"), R("b5", 0, 16), A.is_gt)
+        for j in range(3):
+            tt(R("PRD", 16 * j, 16 * j + 16), R("FST"), R("WKL", 16 * j, 16 * j + 16), A.mult)
+        chain(R("b6", 0, 1), [(sh("BASEH", r), R("PRD", r, r + 1)) for r in range(16)])
+        chain(R("b5", 0, 16), [(R("IH"), R("UPM")), (R("GSELH"), R("PRD", 0, 16))])
+        ts(R("EQ", 0, 16), R("b5", 0, 16), R("b6", 0, 1), A.is_equal)
+        ts(R("EQ", 16, 17), R("PT", 0, 1), PM, A.add, 15.5, A.is_lt)
+        red(R("BAD"), R("EQ"), A.max)
+        ts(R("TG", 0, 1), R("JNK"), R("BAD"), A.mult, R("b6", 0, 1), A.max)
+        chain(R("b7", 128, 144), [(R("PL0"), R("PRD", 16, 32)), (R("PL1"), R("PRD", 32, 48))])
+        tc("v", R("OKT"), R("b7", 128, 144))
+        tt(R("NK"), X("HTS", 0, V + 32, "TG", 0, 1), R("OKT"), A.add)
+        tc("v", X("HT", 0, V + 32, "TG", 0, 1), R("NK"))
+        if t < RO - 1:
+            ts(cc(0), z, -256.0, A.is_ge)
+            chain(R("b7", 64, 64 + NC), [(R("ON"), cc(0)), (R("ONN"), cc(2))])
+            red(R("BS"), R("b7", 64, 64 + NC), A.add)
+            tc("v", R("BI", 0, 1), R("BS"))
+            ts(R("BI", 1, 2), R("BI", 0, 1), 255, A.bitwise_and)
+            ts(R("TB"), R("BI", 1, 2), -1.0, A.mult, R("THF"), A.add)
+        rx = lambda j: R("RX", 48 * j, 48 * j + 48)
+        slots = R("P2", 0, SL)
+        mm([(R("b0", 0, 48), R("GCT"), slots, True, True), (R("b0", 48, 96), R("GA"), slots, True, True)])
+        mm([(R("b1", 0, 48), R("GUU"), slots, True, True), (R("b1", 48, 96), R("GAA"), slots, True, True)])
+        tc("v", rx(0), R("b0", 0, 48))
+        tc("v", R("RL", 48, 96), R("b0", 48, 96))
+        ts(rx(1), rx(0), 1023, A.bitwise_and)
+        tc("v", R("RL", 0, 48), rx(1))
+        tc("s", R("XA"), X("XS", 0, V, "RL", 48, 96))
+        tc("s", R("HEG"), X("HE", V * t, V * t + V, "RL", 0, 48))
+        tc("v" if t == RO - 1 else "s", R("MX"), X("XE", V * t, V * t + V, "RL", 0, 48))
+        for h in range(2):
+            a, b = 384 * h, 384 * h + 384
+            o = R("b%d" % (2 + h), 0, 384)
+            chain(o, [(R("NID"), R("XA", a, b)), (R("ID"), R("MX", a, b))])
+            act(R("GAB", a, b), o, ActivationFunctionType.Abs)
+        tc("s", R("RU"), R("b1", 0, 96))
+        rb = lambda j: R("RB", 48 * j, 48 * j + 48)
+        rf = lambda j: R("RF", 48 * j, 48 * j + 48)
+        act(rb(0), X("FB", 0, LN, "LJ", 0, 3), ActivationFunctionType.Relu)
+        ts(rb(1), R("CX", 0, 48), R("PT", 1, 2), A.is_lt)
+        tt(rb(2), rb(0), rb(1), A.mult)
+        chain(R("b1", 0, 3), wrap("BA", "P2", 0, SL))
+        tc("v", R("RL", 96, 99), R("b1", 0, 3))
+        tc("v", rf(0), X("WD", 0, V, "RL", 96, 99))
+        for h in range(2):
+            a, b = 384 * h, 384 * h + 384
+            o = R("b%d" % (2 + h), 0, 384)
+            chain(o, [(R("ID"), R("MC")), (R("GHE"), R("HEG", a, b)), (R("G16"), R("GAB", a, b))])
+            scan(R("KS", a, b), R("RST"), o, 1000000.0, A.add, A.min)
+        tc("v", rx(2), R("KS", 15, 768, 16))
+        ts(rx(3), rx(2), 15, A.bitwise_and)
+        tt(rx(4), rx(3), R("RU", 0, 48), A.mult)
+        tt(rx(5), rx(4), R("RU", 48, 96), A.add)
+        ts(rx(3), rx(5), 1023, A.bitwise_and)
+        tc("v", R("RH"), rx(3))
+        chain(R("b1", 0, 3), [(sh("BH0", r), R("RH", r, 48, 16)) for r in range(16)])
+        ts(rb(0), rx(2), 0.0, A.is_lt)
+        tt(rb(1), rb(0), rb(2), A.mult)
+        tc("v", R("RL", 100, 103), R("b1", 0, 3))
+        tt(rf(1), X("WE", V * t, V * t + V, "RL", 100, 103), rf(0), A.subtract)
+        tt(rf(2), rf(1), rb(1), A.mult)
+        last = t == RO - 1
+        if last:
+            tc("v", R("YM"), R("WD"))
+        new = rf(1) if last else R("WN")
+        tt(new, rf(2), rf(0), A.add)
+        tc("v", X("YM" if last else "WD", 0, V, "RL", 96, 99), new)
+    store("y", "ym", R("YM"), "oym")
+    for j, m in ((0, "WC0"), (1, "OH6")):
+        ts(R("EQ", 8 * j, 8 * j + 8), R("CX", 0, 8), PG, A.is_equal)
+        ts(R("NEWP", 8 * j, 8 * j + 8), R("EQ", 8 * j, 8 * j + 8), c1("WC", 0) if j == 0 else oh(6), A.mult)
+        for h in range(2):
+            o = R("b%d" % (4 + 2 * j + h), 0, 512, p=8)
+            chain(o, [(R("NEWP", 8 * j, 8 * j + 8), R("HT", 512 * h, 512 * h + 512))])
+            tc("v" if h else "s", R("Y8", V * j + 512 * h, V * j + 512 * h + 512), o)
+        store("y", "yh" if j == 0 else "yv", R("Y8", V * j, V * j + V), "oyh" if j == 0 else "oyv")
+    return ops
+
+
+def link(ops):
+    seen = {}
+    for j, o in enumerate(ops):
+        deps = {}
+
+        def need(i, w):
+            deps[i] = deps.get(i, False) or w
+        for wrt, regs in ((False, o["rd"]), (True, o["wr"])):
+            for n, a, b in regs:
+                bank = SCRATCH[n][0] == "psum"
+                for (i, ia, ib, iw) in seen.get(n, []):
+                    if i == j:
+                        continue
+                    same = ops[i]["q"] == o["q"] and o.get("kind") is None and ops[i].get("kind") is None
+                    over = ia < b and a < ib
+                    if over and (wrt or iw):
+                        if same:
+                            need(i, o["q"] != "t")
+                        else:
+                            need(i, True)
+                    elif bank:
+                        need(i, not same)
+        for wrt, regs in ((False, o["rd"]), (True, o["wr"])):
+            for n, a, b in regs:
+                lst = seen.setdefault(n, [])
+                if wrt:
+                    bank = SCRATCH[n][0] == "psum"
+                    lst[:] = [e for e in lst if e[0] == j or not (a <= e[1] and e[2] <= b)]
+                lst.append((j, a, b, wrt))
+        o["deps"] = deps
+    return ops
+
+
+def order(ops):
+    n = len(ops)
+    nxt = [[] for _ in range(n)]
+    for j, o in enumerate(ops):
+        for i in o["deps"]:
+            nxt[i].append(j)
+    rank = [0.0] * n
+    for i in range(n - 1, -1, -1):
+        best = 0.0
+        for j in nxt[i]:
+            best = max(best, rank[j] + (WAKE if ops[j]["deps"][i] else 0.0))
+        rank[i] = ops[i]["cost"] + ops[i]["lat"] + best
+    rank = [x + AMP * ((i * 7919 + SEED * 104729) * 2654435761 % 65536) / 65536.0 for i, x in enumerate(rank)]
+    left = [len(o["deps"]) for o in ops]
+    ready = [0.0] * n
+    pend = {}
+    for i, o in enumerate(ops):
+        if left[i] == 0:
+            pend.setdefault(o["q"], []).append(i)
+    free = {}
+    seq = []
+    while len(seq) < n:
+        pick = None
+        for q, lst in pend.items():
+            if not lst:
+                continue
+            f = free.get(q, 0.0) if q is not None else 0.0
+            s = min(max(f, ready[i]) for i in lst)
+            best = max((i for i in lst if max(f, ready[i]) <= s + 0.04), key=lambda i: rank[i])
+            s = max(f, ready[best])
+            if pick is None or s < pick[0]:
+                pick = (s, q, best)
+        s, q, i = pick
+        pend[q].remove(i)
+        o = ops[i]
+        o["start"] = s
+        end = s + o["cost"]
+        free[q] = end
+        seq.append(i)
+        for j in nxt[i]:
+            e = ops[j]["deps"][i]
+            ready[j] = max(ready[j], end + o["lat"] + WAKE if e else s)
+            left[j] -= 1
+            if left[j] == 0:
+                pend.setdefault(ops[j]["q"], []).append(j)
+    return seq
+
+
+QSEM = {"v": "sv", "s": "ss", "t": "st", "g": "sg"}
+
+
+def waits(ops, seq):
+    for o in ops:
+        o["sig"] = False
+    for o in ops:
+        for i, w in o["deps"].items():
+            if w:
+                ops[i]["sig"] = True
+    count, know, value = {}, {}, {}
+    total = {}
+    for i in seq:
+        o = ops[i]
+        q = o["q"]
+        k = know.setdefault(q, {}) if q is not None else {}
+        wl = {}
+        for d in sorted(o["deps"], key=lambda d: -ops[d]["start"]):
+            if not o["deps"][d]:
+                continue
+            sem, val = value[d]
+            if k.get(sem, 0) >= val:
+                continue
+            wl[sem] = max(wl.get(sem, 0), val)
+            k[sem] = max(k.get(sem, 0), val)
+            for s2, v2 in ops[d]["knows"].items():
+                k[s2] = max(k.get(s2, 0), v2)
+        o["waits"] = wl
+        o["knows"] = dict(k)
+        if o.get("kind") is not None:
+            value[i] = (o["sem"], 1)
+            total[o["sem"]] = 1
+        elif o["sig"]:
+            sem = QSEM[q]
+            count[sem] = count.get(sem, 0) + o["incs"]
+            value[i] = (sem, count[sem])
+            total[sem] = count[sem]
+        if i in value:
+            o["knows"][value[i][0]] = value[i][1]
+    return total
+
+
+PLAN = {}
+
+
+def plan():
+    if not PLAN:
+        ops = link(make_program())
+        seq = order(ops)
+        PLAN["ops"], PLAN["seq"], PLAN["total"] = ops, seq, waits(ops, seq)
+    return PLAN["ops"], PLAN["seq"], PLAN["total"]
+
+
+def rank_program(g, core, T, topo):
+    rank = T.rank_of(core)
+    if rank is None:
+        return
+    ops, seq, total = plan()
+    queue = {"v": g.vector, "s": g.scalar, "t": g.tensor, "g": g, "y": g.sync}
+
+    def full(sem, val):
+        if sem in ("sv", "ss", "st", "sg"):
+            return val
+        if sem[:2] == "ld" or sem[0] == "o":
+            return 16
+        t = int(sem[4])
+        if sem[:3] == "arr":
+            src = T.cores[(rank + 1 + t) % N]
+            return len(topo.engines(src, core))
+        return len(topo.engines(core, T.cores[(rank - 1 - t) % N]))
+
+    for i in seq:
+        o = ops[i]
+        if o["q"] is None:
+            continue
+        for sem in o["waits"]:
+            queue[o["q"]].wait_ge(T.sem[sem], full(sem, o["waits"][sem]))
+        kind = o.get("kind")
+        if kind == "send":
+            k, t, src = o["call"]
+            dst = T.cores[(rank - 1 - t) % N]
+            rid, pid, _ = topo.addr(dst)
+            g.remote_dma(ap(T, R({"X": "XE", "H": "HE", "W": "WE"}[k], V * t, V * t + V)), ap(T, src),
+                         T.sem["arr%s%d" % (k, t)], T.sem["loc%s%d" % (k, t)], pid, rid, topo.mask(core, dst))
+        elif kind == "dma":
+            o["call"](g, T).then_inc(T.sem[o["sem"]], 16)
+        elif o["q"] == "t":
+            o["call"](g, T, T.sem["st"] if o["sig"] else None)
+        else:
+            c = o["call"](g, T)
+            if o["sig"]:
+                c.then_inc(T.sem[QSEM[o["q"]]], 1)
+    for sem in total:
+        g.wait_ge(T.sem[sem], full(sem, total[sem]))

@@ -5,13 +5,14 @@ N = 6
 V, TY, LN, SL, RT, RO, ST = 1024, 2048, 384, 48, 16, 4, 320
 CH = [112, 112, 96, 64]
 HV = [0]
-SPLIT = [(0, 64)]
 NC = LN // 16
 BW = 144
 NB = V // 16
 
 BUFS = {
-    "WD": (V, "int32"), "XS": (V, "bfloat16"), "RQ": (TY, "int32"), "SS": (TY + 16, "bfloat16"), "THI": (1, "int32"),
+    "WD": (V, "float32"), "WDI": (V, "int32"), "HTV": (V, "bfloat16"), "VP": (V, "bfloat16"), "V16L": (64, "bfloat16"),
+    "HTP": (V, "bfloat16"), "OHB": (128, "bfloat16"), "OHI": (64, "bfloat16"), "VLD": (1, "float32"), "TW8": (1, "float32"), "TG3": (16, "float32"),
+    "CM": (128, "bfloat16"), "G16H": (128, "float16"), "XS": (V, "bfloat16"), "RQ": (TY, "int32"), "SS": (TY + 16, "bfloat16"), "THI": (1, "int32"),
     "HYB": (64, "int32"), "VFB": (64, "int32"), "HT": (V + 32, "bfloat16"), "PERM": (V, "bfloat16"),
     "PERMK": (LN, "bfloat16"), "PLD": (LN, "bfloat16"), "P2": (LN, "bfloat16"), "NEWP": (LN, "bfloat16"),
     "K16": (LN, "uint16"), "W16": (LN, "uint16"), "KF": (LN, "float16"), "WF": (LN, "float16"),
@@ -22,7 +23,7 @@ BUFS = {
     "GSEL": (128, "bfloat16"), "GSELN": (128, "bfloat16"), "GSELH": (128, "float16"),
     "BASE": (BW, "bfloat16"), "BASEH": (BW, "float16"), "BH0": (BW, "float16"), "WR": (16 * BW, "bfloat16"),
     "BE": (BW, "bfloat16"), "BA": (BW, "bfloat16"), "BSX": (BW, "bfloat16"), "BJ": (BW, "bfloat16"), "BV": (BW, "bfloat16"),
-    "BVN": (BW, "bfloat16"), "B2": (BW, "bfloat16"), "BM1": (BW, "bfloat16"), "B16": (BW, "bfloat16"), "BHF": (BW, "bfloat16"), "NID": (128, "bfloat16"), "IKP": (128, "bfloat16"),
+    "NIK": (128, "bfloat16"), "NX": (NC, "bfloat16"), "B2": (BW, "bfloat16"), "BM1": (BW, "bfloat16"), "B16": (BW, "bfloat16"), "BHF": (BW, "bfloat16"), "NID": (128, "bfloat16"), "IKP": (128, "bfloat16"),
     "HTS": (V + 32, "bfloat16"), "GAB": (768, "bfloat16"), "BU": (BW, "bfloat16"),
     "GA": (128, "bfloat16"), "GUU": (128, "bfloat16"), "GAA": (128, "bfloat16"), "GCT": (128, "bfloat16"),
     "G16": (128, "bfloat16"), "GHE": (128, "bfloat16"),
@@ -39,14 +40,13 @@ BUFS = {
     "CC": (4 * NC, "bfloat16"), "PRO": (72, "bfloat16"), "OX": (NC, "bfloat16"), "CP": (128, "bfloat16"), "MU": (72, "float16"), "OF2": (NC, "uint16"),
     "PT": (2, "float32"), "HL": (6 * NC, "int32"), "HLV": (72, "bfloat16"),
     "LJ": (NC, "uint16"), "JP": (2, "uint16"), "GI": (16, "int32"), "OT": (16, "bfloat16"), "FST": (16, "bfloat16"),
-    "WKL": (48, "int32"), "PRD": (48, "float16"), "TWC": (1, "float32"), "EQ": (17, "float32"), "BAD": (1, "float32"), "TG": (2, "uint16"),
+    "WKL": (64, "int32"), "PRD": (64, "float16"), "TWC": (1, "float32"), "EQ": (17, "float32"), "BAD": (1, "float32"), "TG": (2, "uint16"),
     "OKT": (16, "bfloat16"), "NK": (16, "bfloat16"), "BS": (1, "float32"), "BI": (2, "int32"), "TB": (1, "float32"),
-    "RX": (48 * 6, "int32"), "RU": (96, "float32"), "RB": (48 * 3, "bfloat16"), "RF": (48 * 3, "float32"), "RH": (48, "float16"),
-    "RL": (104, "uint16"), "XA": (768, "bfloat16"), "HEG": (768, "bfloat16"), "MX": (768, "bfloat16"), "KS": (768, "float32"), "WN": (48, "int32"),
-    "YM": (V, "float32"), "Y8": (2 * V, "float32"),
+    "RX": (48 * 6, "int32"), "RU": (96, "float32"), "RB": (48 * 4, "bfloat16"), "RF": (48 * 4, "float32"), "RH": (48, "float16"),
+    "RL": (104, "uint16"), "XA": (768, "bfloat16"), "HEG": (768, "bfloat16"), "MX": (768, "bfloat16"), "KS": (768, "int32"), "Y8": (2 * V, "float32"),
 }
 PARTS = {"QT": 48, "SC": 48, "NT": 64, "CT16": 64, "CP": 48, "Y8": 8}
-PACKED = ["CG", "GSEL", "GSELN", "GSELH", "BASE", "BASEH", "BH0", "WR", "BE", "BA", "BSX", "BJ", "BV", "BVN", "B2", "BM1", "B16", "BHF", "NID", "IKP", "BU",
+PACKED = ["CG", "GSEL", "GSELN", "GSELH", "BASE", "BASEH", "BH0", "WR", "BE", "BA", "BSX", "BJ", "BV", "NIK", "B2", "BM1", "B16", "BHF", "NID", "IKP", "BU",
           "GA", "GUU", "GAA", "GCT", "G16", "GHE", "TGE", "TST", "TSN", "PL0", "PL1", "ID", "IH", "NIH", "IKH", "I8", "NI8",
           "I22", "NI22", "ON", "ONN", "D2", "D3", "D7", "D8", "MC", "QC", "QT", "SC", "NT", "JV", "JC", "RR", "RC", "UPM", "JNK", "PF", "OH", "WC"]
 PLACE = {}
@@ -63,13 +63,14 @@ for _n in BUFS:
         SCRATCH[_n] = ("sbuf", [PARTS.get(_n, 128), _c], _d)
 SCRATCH["XE"] = ("sbuf", [128, RO * V], "bfloat16")
 SCRATCH["HE"] = ("sbuf", [128, RO * V], "bfloat16")
-SCRATCH["WE"] = ("sbuf", [128, RO * V], "int32")
+SCRATCH["WE"] = ("sbuf", [128, RO * V], "float32")
 for _i in range(8):
     SCRATCH["b%d" % _i] = ("psum", [128, 512], "float32")
 
 LOADS = ["WD", "XS", "RQ", "SS", "THI", "HYB", "VFB"]
-SEMAPHORES = ["sv", "ss", "st", "sg", "oym", "oyh", "oyv"] + ["ld" + n for n in LOADS]
+SEMAPHORES = ["sv", "ss", "st", "sg", "oym", "oyh", "oyv", "vp0", "vp1", "vp2"] + ["ld" + n for n in LOADS]
 for _t in range(RO):
+    SEMAPHORES += ["ln7%d" % _t, "ln8%d" % _t]
     for _k in ("X", "H", "W"):
         SEMAPHORES += ["arr%s%d" % (_k, _t), "loc%s%d" % (_k, _t)]
 
@@ -77,7 +78,35 @@ A = AluOpType
 CYC = 0.83 * 1.25
 GET, PUT, WAKE = 1.6, 3.8, 0.1
 PEC = 0.417 * 1.25
-SEED, AMP = 0, 0.0
+PRIO = {
+    "D13": 13, "i165": -7, "C4": 0, "F9": 0, "i180": -12, "A10": 5, "B3": 10, "B9": -5, "F30": -2, "F3": -9, "K5": -12, "D31": -11,
+    "B29": 0, "i32": 12, "LF16": 7, "LG7": -11, "F21": 5, "G2": 11, "B37": -21, "LD29": 8, "i71": -6, "LF10": -10, "D11": 3, "i124": 1,
+    "i39": -10, "LB7": -2, "LB52": 8, "LB62": 3, "F41": 12, "LB65": 5, "LG12": 4, "i74": -15, "LF13": 11, "LB28": -3, "LB63": 3,
+    "D2": 23, "LD34": -3, "LF43": 13, "LB51": 7, "F10": -8, "LF22": 10, "LB13": -8, "i13": 11, "B49": 0, "i57": 9, "B36": 4, "i114": 11,
+    "LD18": -11, "B60": -5, "D21": 2, "LB34": -8, "LD32": -15, "LD14": 1, "LD2": -5, "LB24": 8, "LG9": 20, "i170": -7, "i6": 3,
+    "B51": -2, "LC0": 2, "LF26": 3, "F22": 4, "LD0": 11, "D36": 21, "D9": 9, "i51": -4, "i194": -2, "LF42": -9, "i206": 9, "i196": -2,
+    "LB14": -3, "i8": 6, "D35": 11, "D1": -4, "B62": -1, "D22": 3, "LB37": 12, "i183": -4, "B22": 9, "LF35": 8, "E1": 17, "i80": 6,
+    "LA0": -4, "D12": -9, "LB56": 4, "F34": 4, "i172": -10, "D8": 13, "B8": 2, "F0": 1, "D37": -10, "E0": -8, "B43": 5, "LF0": 1,
+    "LB15": 2, "i33": 3, "F25": 0, "i113": -17, "LD1": -1, "LF24": 5, "F33": -9, "LB18": -1, "i10": -6, "LD21": -11, "F37": 4, "D3": 3,
+    "i108": -2, "F27": 5, "LF33": 5, "LG13": 8, "F6": -16, "i93": -1, "D5": -6, "i100": -9, "i176": -6, "LD13": 0, "i203": -2,
+    "i59": -7, "D10": 10, "B50": 9, "i95": -5, "i79": 1, "B18": -8, "B55": -2, "D24": -8, "LD30": 9, "LB54": -10, "LD12": 6, "LB4": 1,
+    "D23": 9, "A5": -2, "LB49": 7, "G7": -3, "B38": -6, "A6": 6, "F31": 9, "K4": -9, "F2": 7, "LF6": -3, "B56": -10, "F26": -9, "F8": 5,
+    "F38": 4, "LG4": -11, "i77": -1,
+}
+for _k in "B36 B60 B62 D1 D10 D11 D23 F21 F34 LA0 LB65 LD30 LF10 LF24 LF6 LG4 i113 i6 i80".split():
+    PRIO.pop(_k)
+PRIO.update({
+    "B29": 2, "LD29": 12, "F41": 6, "LF13": 10, "LB28": 0, "LB63": 1, "D2": 38, "F10": -13, "LB13": -19, "D21": 6, "LD32": -23,
+    "LB24": -2, "LD0": 21, "B22": 18, "E1": 19, "F25": 9, "LB18": -11, "F37": 13, "LG13": 11, "LD13": 6, "B50": 8, "B18": -7, "G7": 4,
+    "A6": 12, "B56": -27, "F26": -27, "D20": -17, "LF20": 10, "LB23": -4, "D0": -1, "LB31": -9, "LF30": -3, "LB64": -9, "LD17": 3,
+    "LF17": 12, "B52": 11, "B25": 8, "LA6": 5, "C1": -1, "E3": 5, "F18": 2, "LK3": -2, "LD35": 0, "F11": 3, "C0": 10, "LD3": 0, "G6": 0,
+    "B0": 3, "B53": 5, "B34": 1, "E2": 10, "LB47": 1, "LF2": 9, "F15": 1, "B30": -10, "LF41": 1, "C2": -2, "F0": -1, "D32": 8, "B13": 18,
+    "D28": -5, "F5": -6, "LD15": 8, "LF38": 10, "B23": -11, "B48": 5, "F42": 7, "LF25": -1, "B14": 9, "B2": 7, "LB43": 12, "LG0": 1,
+    "LB61": -9, "LK4": -11, "B11": 2, "F31": 1, "LD26": -8, "F44": 6, "G1": 0, "A7": -9, "D25": -6,
+})
+LATE2 = 0.0
+EARLY = -30.0
+LATE = 9.0
 
 
 def R(name, c0=0, c1=None, step=1, p=None):
@@ -127,6 +156,10 @@ def two(r):
 
 def make_program():
     ops = []
+    late, at = [0.0], ["i", 0, ""]
+
+    def mark(name):
+        at[0], at[1] = at[2] + name, 0
 
     def add(q, call, reads, writes, cost, **kw):
         rd, wr = [], []
@@ -136,7 +169,8 @@ def make_program():
         for r in writes:
             wr += touched(r)
             rd += lists(r)
-        o = {"q": q, "call": call, "rd": rd, "wr": wr, "cost": cost, "incs": 1, "lat": 0.0}
+        o = {"q": q, "call": call, "rd": rd, "wr": wr, "cost": cost, "incs": 1, "lat": 0.0, "late": late[0], "key": "%s%d" % (at[0], at[1])}
+        at[1] += 1
         o.update(kw)
         ops.append(o)
         return o
@@ -238,13 +272,13 @@ def make_program():
     load("y", R("HYB"), "hy", "ldHYB", 2.0)
     load("s", R("XS"), "xs", "ldXS", 3.5)
     load("y", R("VFB"), "vf", "ldVFB", 2.0)
-    load("y", R("WD"), "wd", "ldWD", 6.0)
+    load("y", R("WDI"), "wd", "ldWD", 6.0)
     load("s", R("RQ"), "rq", "ldRQ", 9.0)
     load("y", R("SS", 0, TY), "sg", "ldSS", 9.0)
     load("y", R("THI"), "th", "ldTHI", 3.0)
 
+    add("g", lambda g, T: g.iota(T["PII"][:, 0:1], [[1, 1]], 0, 1), [], [R("PII", 0, 1)], 0.14, late=-50.0)
     add("g", lambda g, T: g.iota(T["CX"][:, :], [[1, LN]], 0, 0), [], [R("CX")], 0.13 + 2 * LN * CYC / 1000)
-    add("g", lambda g, T: g.iota(T["PII"][:, 0:1], [[1, 1]], 0, 1), [], [R("PII", 0, 1)], 0.14)
     for n, pat in (("IA", [[1, 256], [0, 4]]), ("IB", [[0, 256], [1, 4]])):
         add("g", lambda g, T, n=n, pat=pat: g.iota(T[n][:, :], pat, 0, 0, allow_small_or_imprecise_dtypes=True),
             [], [R(n)], 0.13 + 2 * V * CYC / 1000)
@@ -264,18 +298,23 @@ def make_program():
     ts(R("GSEL"), R("CG"), PG, A.is_equal)
     oh = lambda j: c1("OH", j)
     for r in range(16):
-        by(R("WR", r * BW, (r + 1) * BW), R("BASE"), oh(r))
+        if r % 3:
+            ts(R("WR", r * BW, (r + 1) * BW), R("BASE"), oh(r), A.mult)
+        else:
+            by(R("WR", r * BW, (r + 1) * BW), R("BASE"), oh(r))
     ts(c1("WC", 9), PM, 10.0, A.mult, 1.0, A.add)
     ts(R("BU"), R("BASE"), c1("WC", 9), A.mult)
 
     ts(c1("WC", 8), PM, 1.0, A.is_gt, oh(6), A.subtract)
     ts(R("ID"), R("CX", 0, 128), P_, A.is_equal)
-    for k in (2, 3, 7, 8):
+    for k in (2, 3):
         by(R("D%d" % k), R("ID"), oh(k))
 
     sx, uu = R("b0", 0, 64), R("b1", 0, 64)
+    late[0] = EARLY
     chain(sx, [(sh("BASE", b), R("XS", 64 * b, 64 * b + 64)) for b in range(16)])
     chain(uu, [(sh("BU", b), R("XS", 64 * b, 64 * b + 64)) for b in range(16)])
+    late[0] = 0.0
     pc = lambda j: R("PC", 64 * j, 64 * j + 64)
     ti = lambda j: R("TI", 64 * j, 64 * j + 64)
     kinds = [0, 1, 6, 4, 5, 9, 10, 11, 12]
@@ -289,6 +328,7 @@ def make_program():
     for h in range(2):
         mm([(R("b%d" % (4 + h), 64 * b, 64 * b + 64), wr(8 * h + b, 6), R("PCB", 128, 192), True, True) for b in range(8)])
         tc("s", R("SGA", 512 * h, 512 * h + 512), R("b%d" % (4 + h)))
+    late[0] = EARLY
     tc("v", ti(1), sx)
     split(3, ti(1), 4, 15)
     tc("v", ti(2), uu)
@@ -301,15 +341,20 @@ def make_program():
     ts(ti(0), ti(7), 1023, A.bitwise_and)
     split(7, ti(0), 2, 3)
     tc("v", R("PCB", 192, 576), R("PC", 192, 576))
+    late[0] = 0.0
     fill(R("HT", V, V + 32), 0.0)
     for h in range(2):
         o = R("b%d" % (2 + h))
         mm([(o, R("D2"), R("IA", 512 * h, 512 * h + 512), True, False)])
-        for sub in (kinds[:3], kinds[3:]):
-            mm([(R("b%d" % (2 + h), 64 * b, 64 * b + 64), wr(8 * h + b, k), R("PCB", 64 * kinds.index(k), 64 * kinds.index(k) + 64), False, False)
-                for b in range(8) for k in sub])
+        cell = lambda n, b: R(n, 64 * b, 64 * b + 64)
+        mm([(cell("b%d" % (2 + h), b), wr(8 * h + b, k), cell("PCB", i), False, False) for b in range(8) for i, k in enumerate(kinds[:3])])
         mm([(o, R("D3"), R("IB", 512 * h, 512 * h + 512), False, True)])
-        tc("v" if h else "s", R("HT", 512 * h, 512 * h + 512), R("b%d" % (2 + h)))
+        tc("v" if h else "s", R("HTP", 512 * h, 512 * h + 512), o)
+    for h in range(2):
+        o = R("b%d" % h)
+        mm([x for b in range(8) for x in [(cell("b%d" % h, b), R("ID"), cell("HTP", 8 * h + b), True, False)] +
+            [(cell("b%d" % h, b), wr(8 * h + b, k), cell("PCB", i), False, i == 8) for i, k in enumerate(kinds) if i > 2]])
+        tc("s", R("HT", 512 * h, 512 * h + 512), o)
     by(R("HTS"), R("HT"), c1("WC", 8))
 
     def wcol(j, a, x, b, y):
@@ -325,9 +370,8 @@ def make_program():
     wcol(4, 9, 8, 10, 1)
     wcol(5, 11, 4, 12, 1)
     ts(c1("WC", 6), oh(6), -131072.0, A.mult)
-    ts(c1("WC", 7), oh(6), -1024.0, A.mult)
     for n, s in (("BV", oh(6)), ("BE", c1("WC", 0)), ("BA", c1("WC", 1)), ("BSX", c1("WC", 2)), ("BJ", c1("WC", 3)),
-                 ("BVN", c1("WC", 7)), ("B2", 2.0), ("BM1", -1.0), ("B16", 16.0), ("BHF", 0.5)):
+                 ("B2", 2.0), ("BM1", -1.0), ("B16", 16.0), ("BHF", 0.5)):
         by(R(n), R("BASE"), s)
     ts(R("CT1", 0, 128), R("C15", 0, 128), PM, A.is_le)
     tt(R("TGE"), R("CT1", 0, 128), R("GSEL"), A.mult)
@@ -336,7 +380,7 @@ def make_program():
     ts(R("TSN"), R("TST"), -1.0, A.mult)
     for n, s in (("IH", 1.0), ("NIH", -1.0), ("IKH", 1024.0)):
         ts(R(n), R("ID"), s, A.mult)
-    for n, s in (("NID", -1.0), ("I8", 8192.0), ("NI8", -8192.0), ("I22", 4194304.0), ("NI22", -4194304.0), ("IKP", c1("WC", 8))):
+    for n, s in (("NID", -1.0), ("NIK", -1024.0), ("I8", 8192.0), ("NI8", -8192.0), ("I22", 4194304.0), ("NI22", -4194304.0), ("IKP", c1("WC", 8))):
         by(R(n), R("ID"), s)
     for t in range(RO):
         k = 64 * t
@@ -351,7 +395,6 @@ def make_program():
     ts(R("GSELN"), R("GSEL"), -1.0, A.mult)
     tc("v", R("GSELH"), R("GSEL"))
     tc("v", R("BASEH"), R("BASE"))
-    ts(R("BH0"), R("BASE"), oh(0), A.mult)
     for n, s in (("GA", c1("WC", 1)), ("GUU", c1("WC", 4)), ("GAA", c1("WC", 5)), ("GHE", c1("WC", 6)), ("G16", 16.0)):
         by(R(n), R("GSEL"), s)
     tt(R("NEWP", 0, 128), R("GUU"), R("C15", 0, 128), A.mult)
@@ -373,12 +416,19 @@ def make_program():
     ts(q48("QT", 48, 72), q48("RU", 0, 24), q48("PF", 4, 5), A.add)
     ts(q48("SC", 0, 1), q48("PF", 4, 5), -1.0, A.mult, 1.0, A.add)
     tc("v", q48("SC", 1, 2), q48("PF", 4, 5))
-    ts(R("UPM"), R("CX", 0, 16), PM, A.is_le, 4096.0, A.mult)
+    ts(R("EQ", 0, 16), R("CX", 0, 16), PM, A.is_le, 4096.0, A.mult)
+    ts(R("TG3"), R("OH"), 4096.0, A.mult)
+    tt(R("UPM"), R("EQ", 0, 16), R("TG3"), A.add)
+    ts(R("CT1", 256, 384), R("C15", 0, 128), 1.0, A.add)
+    tt(R("CT2", 256, 384), R("CT1", 256, 384), R("GSEL"), A.mult)
+    ts(R("CM"), R("CT2", 256, 384), -1.0, A.add)
+    ts(R("G16H"), R("GSEL"), 16.0, A.mult)
     ts(R("JNK"), PM, 1032.0, A.add)
     fill(R("SS", TY, TY + 16), 0.0)
     ts(R("THF"), R("THI"), -1.0, A.mult, -8192.5, A.add)
     tc("v", R("TB"), R("THF"))
 
+    tc("v", R("WD"), R("WDI"))
     send("H", 0, R("HT", 0, V))
     send("X", 0, R("XS"))
     send("W", 0, R("WD"))
@@ -394,15 +444,19 @@ def make_program():
             send("H", t, R("HT", 0, V))
             send("W", t, R("WD"))
         kt = 64 * t
-        chain(R("b5", 0, 64), wrap("BV", "HT" if t else "SGA", 0, V))
-        tc("v", R("V16"), R("b5", 0, 64))
-        tt(R("VJ"), R("b5", 0, 64), R("JC", kt, kt + 64), A.mult)
+        at[2] = "L" if t == RO - 1 else ""
+        if t == 0:
+            chain(R("b5", 0, 64), wrap("BV", "SGA", 0, V))
+            tc("v", R("V16"), R("b5", 0, 64))
+        else:
+            tt(R("V16"), R("V16L"), R("b7", 192, 256), A.is_gt)
+        mark("A")
+        tt(R("VJ"), R("V16"), R("JC", kt, kt + 64), A.mult)
         chain(R("b6", 0, 128, p=64), [(R("V16"), R("GSEL"))])
         tc("v", R("CT16"), R("b6", 0, 128, p=64))
         chain(R("b5", 0, 64), [(R("IH"), R("JV", kt, kt + 64)), (R("TGE"), R("V16")), (R("IH"), R("VJ")), (R("CT16"), R("NT", kt, kt + 64))])
         tc("v", R("OFF"), R("b5", 0, 64))
-        for a, b in SPLIT:
-            tc("v", X("PERM", 0, V, "OFF", a, b), R("HT", 16 * a, 16 * b))
+        tc("v", X("PERM", 0, V, "OFF", 0, 64), R("HT" if t else "HTP", 0, V))
         chain(R("b6", 0, NC), wrap("BE", "PERM", 0, LN))
         tc("v", R("Y16"), R("b6", 0, NC))
         chain(R("b5", 0, NC), wrap("BA", "PERM", 0, LN))
@@ -411,13 +465,25 @@ def make_program():
             tc("v", R("K16", 16 * a, 16 * b), X("RQ", 0, TY, "Y16", a, b))
         for a, b in ((0, 8), (8, NC)):
             tc("v", R("W16", 16 * a, 16 * b), X("WD", 0, V, "A16", a, b))
+        mark("Z")
+        if t == 0:
+            tc("s", R("PERM", 0, LN), X("HT", 0, V, "A16", 0, NC))
+        mark("K")
         tc("v", R("KF"), R("K16"))
         tc("v", R("WF"), R("W16"))
         ts(R("DAT"), R("K16"), 2048.0, A.is_ge)
-        chain(R("b4", 0, LN), [(R("ID"), R("PERM", 0, LN)), (R("D7"), R("IA", 0, LN)), (R("D8"), R("IB", 0, LN))])
-        tc("s", R("PLD"), R("b4", 0, LN))
-        z, nn = R("b7", 0, NC), R("b7", NC, 2 * NC)
-        chain(z, wrap("BVN", "PERM", 0, LN) + wrap("BM1", "DAT", 0, LN), last=False)
+        for k, n in ((7, "IA"), (8, "IB")):
+            add("y", lambda g, T, k=k, n=n: g.sync.dma_start(out=T["PERM"][k:128:16, 0:LN], in_=T[n][k:128:16, 0:LN]),
+                [R(n, 0, LN)], [R("PERM", 0, LN)], 0.1, kind="dma", sem="ln%d%d" % (k, t), lat=2.5)
+        last = t == RO - 1
+        if not last:
+            add("y", lambda g, T: g.sync.dma_start(out=T["VP"][:, LN:V], in_=T["PERM"][:, LN:V]),
+                [R("PERM", LN, V)], [R("VP", LN, V)], 0.1, kind="dma", sem="vp%d" % t, lat=3.0)
+        mark("B")
+        z, nn = R("b7", 0, NC), R("b2", 0, NC)
+        chain(R("b6", 0, 1), [(R("CT16"), R("ON", 0, 1, p=64))])
+        ts(R("NX"), R("QC", 48, 72), R("b6", 0, 1), A.add, 1023.5, A.is_gt)
+        chain(z, [(R("NIK"), R("NX"))] + wrap("BM1", "DAT", 0, LN), last=False)
         tc("v", R("YI"), R("Y16"))
         hb = lambda j: R("HB", NC * j, NC * j + NC)
         tt(hb(0), R("YI"), R("YI"), A.mult)
@@ -435,7 +501,9 @@ def make_program():
             tt(R("MXA", g0, g1), X("XS", 0, V, "W16", l0, l1), R("SGA", g0, g1), A.max)
             pick = lambda m, n: [(sh(m, p), R(n, g0 + p, g1, 16)) for p in range(16)]
             chain(E, pick("BE", "HGA") + [(R("NIH"), sl("KF"))])
+            late[0] = EARLY
             ts(sl("OTB"), E, 0.0, A.not_equal)
+            late[0] = 0.0
             chain(D, [(R("NI8"), sl("DAT"))] + pick("BM1", "SGA"), last=False)
             chain(D, pick("BSX", "HGA"), first=False, last=False)
             chain(D, pick("B2", "MXA"), first=False, last=False)
@@ -454,6 +522,15 @@ def make_program():
         tt(R("PRO", 48, 72), R("OX"), cc(3), A.add)
         hl = lambda j: R("HL", NC * j, NC * j + NC)
         ts(R("HLV", 48, 72), z, -224.0, A.is_lt)
+        mark("C")
+        mm([(R("b3", r, LN, 16), wr(r, 6), R("HLV", 48, 72), True, True) for r in range(16)])
+        tc("s", R("VP", 0, LN), R("b3", 0, LN))
+        if not last:
+            tc("s", R("HTV"), X("VP", 0, V, "OFF", 0, 64))
+            ts(cc(0), z, -256.0, A.is_ge)
+            chain(R("b7", 64, 128), wrap("BV", "HTV", 0, V))
+            tc("v", R("V16L"), R("b7", 64, 128))
+        mark("D")
         tt(hl(2), nn, hb(3), A.add)
         chain(R("b5", 0, 128, p=48), [(cc(1, 2), R("GSEL")), (cc(2, 2), R("GSELN"))])
         tc("v", R("CP"), R("b5", 0, 128, p=48))
@@ -465,7 +542,7 @@ def make_program():
         tc("v", R("OF2"), R("b5", 0, NC))
         chain(R("b6", 0, 2), [(R("CP"), R("SC"))])
         tc("v", R("PT"), R("b6", 0, 2))
-        tc("v", X("P2", 0, LN, "OF2", 0, NC), R("PLD"))
+        tc("v", X("P2", 0, LN, "OF2", 0, NC), R("PERM", 0, LN))
         ts(hl(3), hl(2), 2047, A.bitwise_and)
         tt(hl(4), hl(3), R("YI"), A.subtract)
         tt(hl(5), hl(4), cc(3), A.mult)
@@ -473,88 +550,97 @@ def make_program():
         ts(hl(0), hl(2), 3, A.arith_shift_right)
         ts(hl(1), hl(2), 7, A.bitwise_and)
         tc("v", R("HLV", 0, 48), R("HL", 0, 48))
-        mm([x for r in range(16) for x in [(R("b4", r, LN, 16), R("IKP"), R("PERM", r, LN, 16), True, False)] +
-            [(R("b4", r, LN, 16), wr(r, k), R("HLV", 24 * i, 24 * i + 24), False, i == 2) for i, k in enumerate((0, 1, 6))]])
+        mm([(R("b4", 0, LN), R("ID"), R("VP", 0, LN), True, False)])
+        for r0 in range(0, 16, 8):
+            mm([(R("b4", r, LN, 16), wr(r, k), R("HLV", 24 * k, 24 * k + 24), False, False) for r in range(r0, r0 + 8) for k in (0, 1)])
+        mm([(R("b4", 0, LN), R("IKP"), R("PERM", 0, LN), False, True)])
         tc("s", R("PERM", 0, LN), R("b4", 0, LN))
-        tc("s", R("HT", 0, V), X("PERM", 0, V, "OFF", 0, 64))
+        if t:
+            tc("s", R("HT", 0, V), X("PERM", 0, V, "OFF", 0, 64))
+        else:
+            tc("v", X("HT", 0, V, "A16", 0, NC), R("PERM", 0, LN))
         chain(R("b6", 0, NC), wrap("BJ", "P2", 0, LN))
         tc("v", R("JP", 0, 1), R("b6", NC - 1, NC))
         tc("v", R("LJ"), R("b6", 0, NC))
         ts(R("OT"), X("QP", 0, LN, "JP", 0, 1), 4194304.0, A.is_ge)
         tc("v", R("GI"), X("QP", 0, LN, "JP", 0, 1))
         chain(R("b5", 0, 16), [(R("TST"), R("OT"))])
-        ts(R("WKL", 0, 16), R("GI"), 1023, A.bitwise_and)
-        ts(R("WKL", 16, 32), R("GI"), 13, A.arith_shift_right, 255, A.bitwise_and)
-        ts(R("WKL", 32, 48), R("GI"), 10, A.arith_shift_right, 7, A.bitwise_and)
+        for j, (s, m) in enumerate(((4, 63), (0, 15), (13, 255), (10, 7))):
+            ts(R("WKL", 16 * j, 16 * j + 16), R("GI"), s, A.arith_shift_right, m, A.bitwise_and)
         tt(R("FST"), R("OT"), R("b5", 0, 16), A.is_gt)
-        for j in range(3):
+        for j in range(4):
             tt(R("PRD", 16 * j, 16 * j + 16), R("FST"), R("WKL", 16 * j, 16 * j + 16), A.mult)
-        chain(R("b6", 0, 1), [(sh("BASEH", r), R("PRD", r, r + 1)) for r in range(16)])
-        chain(R("b5", 0, 16), [(R("IH"), R("UPM")), (R("GSELH"), R("PRD", 0, 16))])
-        ts(R("EQ", 0, 16), R("b5", 0, 16), R("b6", 0, 1), A.is_equal)
+        mark("E")
+        if not last:
+            chain(R("b6", 0, 2), [(sh("BASEH", r), R("PRD", r, 32, 16)) for r in range(16)])
+            ts(R("VLD"), R("PT", 0, 1), PM, A.add, 15.5, A.is_gt)
+            ts(R("OHB"), R("CM"), R("b6", 1, 2), A.is_equal)
+            ts(R("OHI"), R("CX", 0, 64), R("b6", 0, 1), A.is_equal, R("VLD"), A.mult)
+            chain(R("b7", 192, 256), [(R("OHB"), R("OHI"))])
+        mark("F")
+        chain(R("b5", 0, 16), [(R("IH"), R("UPM")), (R("G16H"), R("PRD", 0, 16)), (R("GSELH"), R("PRD", 16, 32))])
+        red(R("TW8"), R("b5", 0, 16), A.max)
+        ts(R("EQ", 0, 16), R("b5", 0, 16), 8192.0, A.add, R("TW8"), A.is_equal)
         ts(R("EQ", 16, 17), R("PT", 0, 1), PM, A.add, 15.5, A.is_lt)
+        ts(R("TWC"), R("TW8"), -8192.0, A.add)
         red(R("BAD"), R("EQ"), A.max)
-        ts(R("TG", 0, 1), R("JNK"), R("BAD"), A.mult, R("b6", 0, 1), A.max)
-        chain(R("b7", 128, 144), [(R("PL0"), R("PRD", 16, 32)), (R("PL1"), R("PRD", 32, 48))])
-        tc("v", R("OKT"), R("b7", 128, 144))
+        ts(R("TG", 0, 1), R("JNK"), R("BAD"), A.mult, R("TWC"), A.max)
+        chain(R("b4", 400, 416), [(R("PL0"), R("PRD", 32, 48)), (R("PL1"), R("PRD", 48, 64))])
+        tc("v", R("OKT"), R("b4", 400, 416))
         tt(R("NK"), X("HTS", 0, V + 32, "TG", 0, 1), R("OKT"), A.add)
         tc("v", X("HT", 0, V + 32, "TG", 0, 1), R("NK"))
-        if t < RO - 1:
-            ts(cc(0), z, -256.0, A.is_ge)
-            chain(R("b7", 64, 64 + NC), [(R("ON"), cc(0)), (R("ONN"), cc(2))])
-            red(R("BS"), R("b7", 64, 64 + NC), A.add)
-            tc("v", R("BI", 0, 1), R("BS"))
-            ts(R("BI", 1, 2), R("BI", 0, 1), 255, A.bitwise_and)
-            ts(R("TB"), R("BI", 1, 2), -1.0, A.mult, R("THF"), A.add)
+        late[0] = LATE
         rx = lambda j: R("RX", 48 * j, 48 * j + 48)
         slots = R("P2", 0, SL)
-        mm([(R("b0", 0, 48), R("GCT"), slots, True, True), (R("b0", 48, 96), R("GA"), slots, True, True)])
-        mm([(R("b1", 0, 48), R("GUU"), slots, True, True), (R("b1", 48, 96), R("GAA"), slots, True, True)])
+        mm([(R("b0", 0, 48), R("GCT"), slots, True, True)])
+        chain(R("b1", 0, 3), wrap("BA", "P2", 0, SL))
         tc("v", rx(0), R("b0", 0, 48))
-        tc("v", R("RL", 48, 96), R("b0", 48, 96))
+        tc("v", R("RL", 96, 99), R("b1", 0, 3))
         ts(rx(1), rx(0), 1023, A.bitwise_and)
         tc("v", R("RL", 0, 48), rx(1))
-        tc("s", R("XA"), X("XS", 0, V, "RL", 48, 96))
-        tc("s", R("HEG"), X("HE", V * t, V * t + V, "RL", 0, 48))
-        tc("v" if t == RO - 1 else "s", R("MX"), X("XE", V * t, V * t + V, "RL", 0, 48))
+        tc("s", R("XA", 0, 48), X("XS", 0, V, "RL", 96, 99))
         for h in range(2):
             a, b = 384 * h, 384 * h + 384
             o = R("b%d" % (2 + h), 0, 384)
-            chain(o, [(R("NID"), R("XA", a, b)), (R("ID"), R("MX", a, b))])
+            q = "v" if last and h == 0 else "s"
+            tc(q, R("MX", a, b), X("XE", V * t, V * t + V, "RL", 24 * h, 24 * h + 24))
+            tc(q, R("HEG", a, b), X("HE", V * t, V * t + V, "RL", 24 * h, 24 * h + 24))
+            mm([x for m in range(16) for x in ((R(o[1], m, 384, 16), R("NID"), R("XA", 24 * h, 24 * h + 24), True, False),
+                                               (R(o[1], m, 384, 16), R("ID"), R("MX", a + m, b, 16), False, True))])
             act(R("GAB", a, b), o, ActivationFunctionType.Abs)
-        tc("s", R("RU"), R("b1", 0, 96))
         rb = lambda j: R("RB", 48 * j, 48 * j + 48)
         rf = lambda j: R("RF", 48 * j, 48 * j + 48)
         act(rb(0), X("FB", 0, LN, "LJ", 0, 3), ActivationFunctionType.Relu)
         ts(rb(1), R("CX", 0, 48), R("PT", 1, 2), A.is_lt)
         tt(rb(2), rb(0), rb(1), A.mult)
-        chain(R("b1", 0, 3), wrap("BA", "P2", 0, SL))
-        tc("v", R("RL", 96, 99), R("b1", 0, 3))
         tc("v", rf(0), X("WD", 0, V, "RL", 96, 99))
         for h in range(2):
             a, b = 384 * h, 384 * h + 384
             o = R("b%d" % (2 + h), 0, 384)
             chain(o, [(R("ID"), R("MC")), (R("GHE"), R("HEG", a, b)), (R("G16"), R("GAB", a, b))])
             scan(R("KS", a, b), R("RST"), o, 1000000.0, A.add, A.min)
-        tc("v", rx(2), R("KS", 15, 768, 16))
-        ts(rx(3), rx(2), 15, A.bitwise_and)
-        tt(rx(4), rx(3), R("RU", 0, 48), A.mult)
-        tt(rx(5), rx(4), R("RU", 48, 96), A.add)
-        ts(rx(3), rx(5), 1023, A.bitwise_and)
-        tc("v", R("RH"), rx(3))
-        chain(R("b1", 0, 3), [(sh("BH0", r), R("RH", r, 48, 16)) for r in range(16)])
-        ts(rb(0), rx(2), 0.0, A.is_lt)
-        tt(rb(1), rb(0), rb(2), A.mult)
+        late[0] = LATE2
+        key = R("KS", 15, 768, 16)
+        ts(rx(3), key, 15, A.bitwise_and)
+        ts(rb(3), rx(3), PM, A.is_equal)
+        tt(R("RH"), rb(3), rx(1), A.mult)
+        chain(R("b1", 0, 3), [(sh("BASEH", r), R("RH", r, 48, 16)) for r in range(16)])
         tc("v", R("RL", 100, 103), R("b1", 0, 3))
-        tt(rf(1), X("WE", V * t, V * t + V, "RL", 100, 103), rf(0), A.subtract)
-        tt(rf(2), rf(1), rb(1), A.mult)
-        last = t == RO - 1
-        if last:
-            tc("v", R("YM"), R("WD"))
-        new = rf(1) if last else R("WN")
-        tt(new, rf(2), rf(0), A.add)
-        tc("v", X("YM" if last else "WD", 0, V, "RL", 96, 99), new)
-    store("y", "ym", R("YM"), "oym")
+        ts(rb(0), key, 0.0, A.is_lt)
+        tt(rb(1), rb(0), rb(2), A.mult)
+        tt(rf(1), rf(0), rb(1), A.mult)
+        tt(rf(2), rf(0), rf(1), A.subtract)
+        tt(rf(3), X("WE", V * t, V * t + V, "RL", 100, 103), rb(1), A.mult)
+        tt(X("WD", 0, V, "RL", 96, 99), rf(3), rf(2), A.add)
+        late[0] = 0.0
+        mark("G")
+        if not last:
+            chain(R("b1", 0, NC), [(R("ON"), cc(0)), (R("ONN"), cc(2))])
+            red(R("BS"), R("b1", 0, NC), A.add)
+            tc("v", R("BI", 0, 1), R("BS"))
+            ts(R("BI", 1, 2), R("BI", 0, 1), 255, A.bitwise_and)
+            ts(R("TB"), R("BI", 1, 2), -1.0, A.mult, R("THF"), A.add)
+    store("y", "ym", R("WD"), "oym")
     for j, m in ((0, "WC0"), (1, "OH6")):
         ts(R("EQ", 8 * j, 8 * j + 8), R("CX", 0, 8), PG, A.is_equal)
         ts(R("NEWP", 8 * j, 8 * j + 8), R("EQ", 8 * j, 8 * j + 8), c1("WC", 0) if j == 0 else oh(6), A.mult)
@@ -611,7 +697,9 @@ def order(ops):
         for j in nxt[i]:
             best = max(best, rank[j] + (WAKE if ops[j]["deps"][i] else 0.0))
         rank[i] = ops[i]["cost"] + ops[i]["lat"] + best
-    rank = [x + AMP * ((i * 7919 + SEED * 104729) * 2654435761 % 65536) / 65536.0 for i, x in enumerate(rank)]
+    def own(k):
+        return PRIO.get(k, PRIO.get(k[1:], 0.0) if k[0] == "L" else 0.0)
+    rank = [x - ops[i]["late"] + own(ops[i]["key"]) for i, x in enumerate(rank)]
     left = [len(o["deps"]) for o in ops]
     ready = [0.0] * n
     pend = {}
@@ -710,7 +798,7 @@ def rank_program(g, core, T, topo):
     def full(sem, val):
         if sem in ("sv", "ss", "st", "sg"):
             return val
-        if sem[:2] == "ld" or sem[0] == "o":
+        if sem[:2] in ("ld", "vp", "ln") or sem[0] == "o":
             return 16
         t = int(sem[4])
         if sem[:3] == "arr":

from concourse.bass import DstId, RemoteDMATransfer
from concourse.mybir import dt, AluOpType, AxisListType, ActivationFunctionType

N = 6
V, TY, LN, SL, RT, RO, ST = 1024, 2048, 384, 48, 16, 4, 320
CH = [112, 112, 96, 64]
HV = [0]
NC = LN // 16
BW = 144
NB = V // 16

BUFS = {
    "WD": (V, "float32"), "WDI": (V, "int32"), "HTV": (V, "bfloat16"), "VP": (V, "bfloat16"), "V16L": (64, "bfloat16"),
    "HTP": (V, "bfloat16"), "OHB": (128, "bfloat16"), "OHI": (64, "bfloat16"), "VLD": (1, "float32"), "TW8": (1, "float32"), "TG3": (16, "float32"),
    "CM": (128, "bfloat16"), "G16H": (128, "float16"), "XS": (V, "bfloat16"), "RQ": (TY, "int32"), "SS": (TY + 16, "bfloat16"), "THI": (1, "int32"),
    "HYB": (64, "int32"), "VFB": (64, "int32"), "HT": (V + 32, "bfloat16"), "PERM": (V, "bfloat16"),
    "PERMK": (LN, "bfloat16"), "PLD": (LN, "bfloat16"), "P2": (LN, "bfloat16"), "NEWP": (LN, "bfloat16"),
    "K16": (LN, "uint16"), "W16": (LN, "uint16"), "KF": (LN, "float16"), "WF": (LN, "float16"),
    "DAT": (LN, "bfloat16"), "OTB": (LN, "bfloat16"), "FB": (LN, "bfloat16"), "QP": (LN, "float32"),
    "SGA": (16 * LN, "bfloat16"), "HGA": (16 * LN, "bfloat16"), "MXA": (16 * LN, "bfloat16"),
    "CX": (LN, "int32"), "C15": (LN, "int32"), "CT1": (LN, "int32"), "CT2": (LN, "int32"), "CG": (128, "int32"), "PII": (16, "int32"),
    "PF": (16, "float32"), "OH": (16, "float32"), "WC": (16, "float32"),
    "GSEL": (128, "bfloat16"), "GSELN": (128, "bfloat16"), "GSELH": (128, "float16"),
    "BASE": (BW, "bfloat16"), "BASEH": (BW, "float16"), "BH0": (BW, "float16"), "WR": (16 * BW, "bfloat16"),
    "BE": (BW, "bfloat16"), "BA": (BW, "bfloat16"), "BSX": (BW, "bfloat16"), "BJ": (BW, "bfloat16"), "BV": (BW, "bfloat16"),
    "NIK": (128, "bfloat16"), "NX": (NC, "bfloat16"), "B2": (BW, "bfloat16"), "BM1": (BW, "bfloat16"), "B16": (BW, "bfloat16"), "BHF": (BW, "bfloat16"), "NID": (128, "bfloat16"), "IKP": (128, "bfloat16"),
    "HTS": (V + 32, "bfloat16"), "GAB": (768, "bfloat16"), "BU": (BW, "bfloat16"),
    "GA": (128, "bfloat16"), "GUU": (128, "bfloat16"), "GAA": (128, "bfloat16"), "GCT": (128, "bfloat16"),
    "G16": (128, "bfloat16"), "GHE": (128, "bfloat16"),
    "TGE": (128, "bfloat16"), "TST": (128, "bfloat16"), "TSN": (128, "bfloat16"), "PL0": (128, "float16"), "PL1": (128, "float16"),
    "ID": (128, "bfloat16"), "IH": (128, "float16"), "NIH": (128, "float16"), "IKH": (128, "float16"),
    "I8": (128, "bfloat16"), "NI8": (128, "bfloat16"), "I22": (128, "bfloat16"), "NI22": (128, "bfloat16"),
    "ON": (128, "bfloat16"), "ONN": (128, "bfloat16"), "IA": (V, "bfloat16"), "IB": (V, "bfloat16"),
    "D2": (128, "bfloat16"), "D3": (128, "bfloat16"), "D7": (128, "bfloat16"), "D8": (128, "bfloat16"), "MC": (LN, "bfloat16"), "RST": (LN, "float32"),
    "QC": (72, "float16"), "QT": (72, "bfloat16"), "SC": (2, "bfloat16"), "NT": (256, "bfloat16"), "JV": (256, "float16"), "JC": (256, "float16"),
    "RR": (256, "int32"), "RC": (8, "int32"), "RCF": (8, "float32"), "UPM": (16, "float16"), "JNK": (1, "float32"),
    "PC": (704, "int32"), "PCB": (704, "bfloat16"), "TI": (512, "int32"), "THF": (1, "float32"),
    "V16": (64, "bfloat16"), "VJ": (64, "float16"), "CT16": (128, "bfloat16"), "OFF": (64, "uint16"),
    "Y16": (NC, "uint16"), "A16": (NC, "uint16"), "YI": (NC, "int32"), "HB": (4 * NC, "int32"),
    "CC": (4 * NC, "bfloat16"), "PRO": (72, "bfloat16"), "OX": (NC, "bfloat16"), "CP": (128, "bfloat16"), "MU": (72, "float16"), "OF2": (NC, "uint16"),
    "PT": (2, "float32"), "HL": (6 * NC, "int32"), "HLV": (72, "bfloat16"),
    "LJ": (NC, "uint16"), "JP": (2, "uint16"), "GI": (16, "int32"), "OT": (16, "bfloat16"), "FST": (16, "bfloat16"),
    "WKL": (64, "int32"), "PRD": (64, "float16"), "TWC": (1, "float32"), "EQ": (17, "float32"), "BAD": (1, "float32"), "TG": (2, "uint16"),
    "OKT": (16, "bfloat16"), "NK": (16, "bfloat16"), "BS": (1, "float32"), "BI": (2, "int32"), "TB": (1, "float32"),
    "RX": (48 * 6, "int32"), "RU": (96, "float32"), "RB": (48 * 4, "bfloat16"), "RF": (48 * 4, "float32"), "RH": (48, "float16"),
    "RL": (104, "uint16"), "XA": (768, "bfloat16"), "HEG": (768, "bfloat16"), "MX": (768, "bfloat16"), "KS": (768, "int32"), "Y8": (2 * V, "float32"),
}
PARTS = {"QT": 48, "SC": 48, "NT": 64, "CT16": 64, "CP": 48, "Y8": 8}
PACKED = ["CG", "GSEL", "GSELN", "GSELH", "BASE", "BASEH", "BH0", "WR", "BE", "BA", "BSX", "BJ", "BV", "NIK", "B2", "BM1", "B16", "BHF", "NID", "IKP", "BU",
          "GA", "GUU", "GAA", "GCT", "G16", "GHE", "TGE", "TST", "TSN", "PL0", "PL1", "ID", "IH", "NIH", "IKH", "I8", "NI8",
          "I22", "NI22", "ON", "ONN", "D2", "D3", "D7", "D8", "MC", "QC", "QT", "SC", "NT", "JV", "JC", "RR", "RC", "UPM", "JNK", "PF", "OH", "WC"]
PLACE = {}
SCRATCH = {}
for _n in BUFS:
    _c, _d = BUFS[_n]
    if _n in PACKED:
        _k = "k" + _d
        _o = SCRATCH[_k][1][1] if _k in SCRATCH else 0
        PLACE[_n] = (_k, _o)
        SCRATCH[_k] = ("sbuf", [128, _o + (_c + 15) // 16 * 16], _d)
    else:
        PLACE[_n] = (_n, 0)
        SCRATCH[_n] = ("sbuf", [PARTS.get(_n, 128), _c], _d)
SCRATCH["XE"] = ("sbuf", [128, RO * V], "bfloat16")
SCRATCH["HE"] = ("sbuf", [128, RO * V], "bfloat16")
SCRATCH["WE"] = ("sbuf", [128, RO * V], "float32")
for _i in range(8):
    SCRATCH["b%d" % _i] = ("psum", [128, 512], "float32")

LOADS = ["WD", "XS", "RQ", "SS", "THI", "HYB", "VFB"]
SEMAPHORES = ["sv", "ss", "st", "sg", "oym", "oyh", "oyv", "vp0", "vp1", "vp2"] + ["ld" + n for n in LOADS]
for _t in range(RO):
    SEMAPHORES += ["ln7%d" % _t, "ln8%d" % _t]
    for _k in ("X", "H", "W"):
        SEMAPHORES += ["arr%s%d" % (_k, _t), "loc%s%d" % (_k, _t)]

A = AluOpType
CYC = 0.83 * 1.25
GET, PUT, WAKE = 1.6, 3.8, 0.1
PEC = 0.417 * 1.25
PRIO = {
    "D13": 13, "i165": -7, "C4": 0, "F9": 0, "i180": -12, "A10": 5, "B3": 10, "B9": -5, "F30": -2, "F3": -9, "K5": -12, "D31": -11,
    "B29": 0, "i32": 12, "LF16": 7, "LG7": -11, "F21": 5, "G2": 11, "B37": -21, "LD29": 8, "i71": -6, "LF10": -10, "D11": 3, "i124": 1,
    "i39": -10, "LB7": -2, "LB52": 8, "LB62": 3, "F41": 12, "LB65": 5, "LG12": 4, "i74": -15, "LF13": 11, "LB28": -3, "LB63": 3,
    "D2": 23, "LD34": -3, "LF43": 13, "LB51": 7, "F10": -8, "LF22": 10, "LB13": -8, "i13": 11, "B49": 0, "i57": 9, "B36": 4, "i114": 11,
    "LD18": -11, "B60": -5, "D21": 2, "LB34": -8, "LD32": -15, "LD14": 1, "LD2": -5, "LB24": 8, "LG9": 20, "i170": -7, "i6": 3,
    "B51": -2, "LC0": 2, "LF26": 3, "F22": 4, "LD0": 11, "D36": 21, "D9": 9, "i51": -4, "i194": -2, "LF42": -9, "i206": 9, "i196": -2,
    "LB14": -3, "i8": 6, "D35": 11, "D1": -4, "B62": -1, "D22": 3, "LB37": 12, "i183": -4, "B22": 9, "LF35": 8, "E1": 17, "i80": 6,
    "LA0": -4, "D12": -9, "LB56": 4, "F34": 4, "i172": -10, "D8": 13, "B8": 2, "F0": 1, "D37": -10, "E0": -8, "B43": 5, "LF0": 1,
    "LB15": 2, "i33": 3, "F25": 0, "i113": -17, "LD1": -1, "LF24": 5, "F33": -9, "LB18": -1, "i10": -6, "LD21": -11, "F37": 4, "D3": 3,
    "i108": -2, "F27": 5, "LF33": 5, "LG13": 8, "F6": -16, "i93": -1, "D5": -6, "i100": -9, "i176": -6, "LD13": 0, "i203": -2,
    "i59": -7, "D10": 10, "B50": 9, "i95": -5, "i79": 1, "B18": -8, "B55": -2, "D24": -8, "LD30": 9, "LB54": -10, "LD12": 6, "LB4": 1,
    "D23": 9, "A5": -2, "LB49": 7, "G7": -3, "B38": -6, "A6": 6, "F31": 9, "K4": -9, "F2": 7, "LF6": -3, "B56": -10, "F26": -9, "F8": 5,
    "F38": 4, "LG4": -11, "i77": -1,
}
for _k in "B36 B60 B62 D1 D10 D11 D23 F21 F34 LA0 LB65 LD30 LF10 LF24 LF6 LG4 i113 i6 i80".split():
    PRIO.pop(_k)
PRIO.update({
    "B29": 2, "LD29": 12, "F41": 6, "LF13": 10, "LB28": 0, "LB63": 1, "D2": 38, "F10": -13, "LB13": -19, "D21": 6, "LD32": -23,
    "LB24": -2, "LD0": 21, "B22": 18, "E1": 19, "F25": 9, "LB18": -11, "F37": 13, "LG13": 11, "LD13": 6, "B50": 8, "B18": -7, "G7": 4,
    "A6": 12, "B56": -27, "F26": -27, "D20": -17, "LF20": 10, "LB23": -4, "D0": -1, "LB31": -9, "LF30": -3, "LB64": -9, "LD17": 3,
    "LF17": 12, "B52": 11, "B25": 8, "LA6": 5, "C1": -1, "E3": 5, "F18": 2, "LK3": -2, "LD35": 0, "F11": 3, "C0": 10, "LD3": 0, "G6": 0,
    "B0": 3, "B53": 5, "B34": 1, "E2": 10, "LB47": 1, "LF2": 9, "F15": 1, "B30": -10, "LF41": 1, "C2": -2, "F0": -1, "D32": 8, "B13": 18,
    "D28": -5, "F5": -6, "LD15": 8, "LF38": 10, "B23": -11, "B48": 5, "F42": 7, "LF25": -1, "B14": 9, "B2": 7, "LB43": 12, "LG0": 1,
    "LB61": -9, "LK4": -11, "B11": 2, "F31": 1, "LD26": -8, "F44": 6, "G1": 0, "A7": -9, "D25": -6,
})
LATE2 = 0.0
EARLY = -30.0
LATE = 9.0


def R(name, c0=0, c1=None, step=1, p=None):
    if c1 is None:
        c1 = BUFS[name][0] if name in BUFS else SCRATCH[name][1][1]
    if p is None:
        p = PARTS.get(name, 128)
    name, o = PLACE.get(name, (name, 0))
    return ("ap", name, c0 + o, c1 + o, step, p)


def X(name, c0, c1, off, o0, o1):
    return ("ind", name, c0, c1, off, o0, o1)


def ap(T, r):
    if r[0] == "ap":
        _, n, c0, c1, step, p = r
        if step == 1:
            return T[n][0:p, c0:c1]
        return T[n][0:p, c0:c1:step]
    _, n, c0, c1, off, o0, o1 = r
    return T[n][:, c0:c1].indirect(T[off][:, o0:o1])


def width(r):
    if r[0] == "ind":
        return 16 * (r[6] - r[5])
    return -(-(r[3] - r[2]) // r[4])


def touched(r):
    return [(r[1], r[2], r[3])]


def lists(r):
    return [(r[4], r[5], r[6])] if r[0] == "ind" else []


def psum(r):
    return r[0] == "ap" and SCRATCH[r[1]][0] == "psum"


def two(r):
    return SCRATCH[r[1]][2] in ("bfloat16", "float16", "uint16") and r[0] == "ap"


def make_program():
    ops = []
    late, at = [0.0], ["i", 0, ""]

    def mark(name):
        at[0], at[1] = at[2] + name, 0

    def add(q, call, reads, writes, cost, **kw):
        rd, wr = [], []
        for r in reads:
            if isinstance(r, tuple):
                rd += touched(r) + lists(r)
        for r in writes:
            wr += touched(r)
            rd += lists(r)
        o = {"q": q, "call": call, "rd": rd, "wr": wr, "cost": cost, "incs": 1, "lat": 0.0, "late": late[0], "key": "%s%d" % (at[0], at[1])}
        at[1] += 1
        o.update(kw)
        ops.append(o)
        return o

    def price(refs, out, mult, q):
        n = max([width(r) for r in refs])
        if out[0] == "ind":
            return 0.05 + PUT * CYC / 1000 * width(out)
        if any(r[0] == "ind" for r in refs):
            return 0.06 + GET * CYC / 1000 * n
        return max(64, n * mult) * CYC / 1000 + (0.01 if q == "v" else 0.06)

    def tc(q, out, in_):
        if q == "v":
            f = lambda g, T: g.vector.tensor_copy(out=ap(T, out), in_=ap(T, in_))
        else:
            f = lambda g, T: g.scalar.activation(ap(T, out), ap(T, in_), ActivationFunctionType.Copy)
        add(q, f, [in_], [out], price([in_, out], out, 0.5 if two(in_) and two(out) and q == "v" else 1, q))

    def act(out, in_, func, bias=None):
        def f(g, T):
            if bias is None:
                return g.scalar.activation(ap(T, out), ap(T, in_), func)
            return g.scalar.activation(ap(T, out), ap(T, in_), func, bias=ap(T, bias))
        add("s", f, [in_, bias], [out], price([in_], out, 1, "s"))

    def by(out, in_, col):
        add("s", lambda g, T: g.scalar.activation(ap(T, out), ap(T, in_), ActivationFunctionType.Copy,
                                                  scale=ap(T, col) if isinstance(col, tuple) else col),
            [in_, col], [out], price([in_], out, 1, "s"))

    def tt(out, a, b, op):
        add("v", lambda g, T: g.vector.tensor_tensor(out=ap(T, out), in0=ap(T, a), in1=ap(T, b), op=op), [a, b], [out],
            price([a, b], out, 1 if psum(a) or psum(b) else 2, "v"))

    def ts(out, a, s1, op0, s2=None, op1=None):
        def f(g, T):
            x1 = ap(T, s1) if isinstance(s1, tuple) else s1
            x2 = ap(T, s2) if isinstance(s2, tuple) else s2
            if op1 is None:
                return g.vector.tensor_scalar(out=ap(T, out), in0=ap(T, a), scalar1=x1, scalar2=None, op0=op0)
            return g.vector.tensor_scalar(out=ap(T, out), in0=ap(T, a), scalar1=x1, scalar2=x2, op0=op0, op1=op1)
        add("v", f, [a, s1, s2], [out], price([a], out, 0.5 if two(a) and two(out) else 1, "v"))

    def red(out, a, op):
        add("v", lambda g, T: g.vector.tensor_reduce(out=ap(T, out), in_=ap(T, a), axis=AxisListType.X, op=op), [a], [out], price([a], out, 1, "v"))

    def scan(out, d0, d1, init, op0, op1):
        add("v", lambda g, T: g.vector.tensor_tensor_scan(out=ap(T, out), data0=ap(T, d0), data1=ap(T, d1), initial=init, op0=op0, op1=op1),
            [d0, d1], [out], price([d0, d1], out, 1, "v"))

    def fill(out, c):
        add("v", lambda g, T: g.vector.memset(ap(T, out), c), [], [out], price([out], out, 1, "v"))

    def mm(items):
        last = len(items) - 1
        sig = [i for i, x in enumerate(items) if x[4] or i == last]

        def f(g, T, sem=None):
            for i, (o, l, r, s, e) in enumerate(items):
                c = g.tensor.matmul(out=ap(T, o), lhsT=ap(T, l), rhs=ap(T, r), start=s, stop=e)
                if sem is not None and i in sig:
                    c.then_inc(sem, 1)
        rd, wr = [], []
        for x in items:
            rd += [x[1], x[2]]
            wr += [x[0]]
        add("t", f, list(dict.fromkeys(rd)), list(dict.fromkeys(wr)), sum(max(64, width(x[2])) for x in items) * PEC / 1000, incs=len(sig))

    def chain(out, pairs, first=True, last=True):
        k = len(pairs) - 1
        mm([(out, l, r, first and i == 0, last and i == k) for i, (l, r) in enumerate(pairs)])

    def sh(name, m):
        return R(name, 15 - m, 15 - m + 128)

    def wr(r, m):
        return R("WR", r * BW + 15 - m, r * BW + 15 - m + 128)

    def wrap(mat, src, c0, c1):
        return [(sh(mat, r), R(src, c0 + r, c1, 16)) for r in range(16)]

    def send(kind, t, src):
        add("g", (kind, t, src), [src], [], 0.3, kind="send", sem="loc%s%d" % (kind, t), lat=6.0)

    def recv(kind, t, dst):
        add(None, None, [], [dst], 0.0, kind="recv", sem="arr%s%d" % (kind, t), lat=14.0 + 30 * t)

    def load(q, dst, name, sem, lat):
        def f(g, T):
            return (g.sync if q == "y" else g.scalar).dma_start(out=ap(T, dst), in_=T[name][:, :])
        add(q, f, [], [dst], 0.1, kind="dma", sem=sem, lat=lat)

    def store(q, name, src, sem):
        def f(g, T):
            return (g.sync if q == "y" else g.scalar).dma_start(out=T[name][:, :], in_=ap(T, src))
        add(q, f, [src], [], 0.1, kind="dma", sem=sem, lat=3.0)

    load("y", R("HYB"), "hy", "ldHYB", 2.0)
    load("s", R("XS"), "xs", "ldXS", 3.5)
    load("y", R("VFB"), "vf", "ldVFB", 2.0)
    load("y", R("WDI"), "wd", "ldWD", 6.0)
    load("s", R("RQ"), "rq", "ldRQ", 9.0)
    load("y", R("SS", 0, TY), "sg", "ldSS", 9.0)
    load("y", R("THI"), "th", "ldTHI", 3.0)

    add("g", lambda g, T: g.iota(T["PII"][:, 0:1], [[1, 1]], 0, 1), [], [R("PII", 0, 1)], 0.14, late=-50.0)
    add("g", lambda g, T: g.iota(T["CX"][:, :], [[1, LN]], 0, 0), [], [R("CX")], 0.13 + 2 * LN * CYC / 1000)
    for n, pat in (("IA", [[1, 256], [0, 4]]), ("IB", [[0, 256], [1, 4]])):
        add("g", lambda g, T, n=n, pat=pat: g.iota(T[n][:, :], pat, 0, 0, allow_small_or_imprecise_dtypes=True),
            [], [R(n)], 0.13 + 2 * V * CYC / 1000)
    c1 = lambda n, j: R(n, j, j + 1)
    P_, PM, PG, P15, K24, PM24, P64 = [c1("PF", j) for j in range(7)]
    ts(c1("PII", 1), c1("PII", 0), 15, A.bitwise_and)
    ts(c1("PII", 2), c1("PII", 0), 4, A.arith_shift_right)
    tc("v", R("PF", 0, 3), R("PII", 0, 3))
    ts(P15, PG, 16.0, A.mult, 15.0, A.add)
    ts(K24, P_, 24.0, A.is_ge)
    ts(PM24, P_, -24.0, A.add)
    ts(P64, PM, 64.0, A.mult)
    ts(R("C15"), R("CX"), 15, A.bitwise_and)
    ts(R("CG"), R("CX", 0, 128), 4, A.arith_shift_right)
    ts(R("OH"), R("C15", 0, 16), PM, A.is_equal)
    ts(R("BASE"), R("CX", 0, BW), P15, A.is_equal)
    ts(R("GSEL"), R("CG"), PG, A.is_equal)
    oh = lambda j: c1("OH", j)
    for r in range(16):
        if r % 3:
            ts(R("WR", r * BW, (r + 1) * BW), R("BASE"), oh(r), A.mult)
        else:
            by(R("WR", r * BW, (r + 1) * BW), R("BASE"), oh(r))
    ts(c1("WC", 9), PM, 10.0, A.mult, 1.0, A.add)
    ts(R("BU"), R("BASE"), c1("WC", 9), A.mult)

    ts(c1("WC", 8), PM, 1.0, A.is_gt, oh(6), A.subtract)
    ts(R("ID"), R("CX", 0, 128), P_, A.is_equal)
    for k in (2, 3):
        by(R("D%d" % k), R("ID"), oh(k))

    sx, uu = R("b0", 0, 64), R("b1", 0, 64)
    late[0] = EARLY
    chain(sx, [(sh("BASE", b), R("XS", 64 * b, 64 * b + 64)) for b in range(16)])
    chain(uu, [(sh("BU", b), R("XS", 64 * b, 64 * b + 64)) for b in range(16)])
    late[0] = 0.0
    pc = lambda j: R("PC", 64 * j, 64 * j + 64)
    ti = lambda j: R("TI", 64 * j, 64 * j + 64)
    kinds = [0, 1, 6, 4, 5, 9, 10, 11, 12]

    def split(j, src, s, m):
        ts(pc(j), src, s, A.arith_shift_right)
        ts(pc(j + 1), src, m, A.bitwise_and)
    split(0, R("HYB"), 3, 7)
    tc("v", pc(2), R("VFB"))
    tc("v", R("PCB", 0, 192), R("PC", 0, 192))
    for h in range(2):
        mm([(R("b%d" % (4 + h), 64 * b, 64 * b + 64), wr(8 * h + b, 6), R("PCB", 128, 192), True, True) for b in range(8)])
        tc("s", R("SGA", 512 * h, 512 * h + 512), R("b%d" % (4 + h)))
    late[0] = EARLY
    tc("v", ti(1), sx)
    split(3, ti(1), 4, 15)
    tc("v", ti(2), uu)
    ts(ti(3), ti(2), 1023, A.bitwise_and)
    ts(ti(4), ti(3), 2.0, A.mult, 1.0, A.add)
    split(5, ti(4), 3, 7)
    tt(ti(5), ti(3), ti(3), A.mult)
    ts(ti(6), ti(5), 5, A.arith_shift_right)
    tt(ti(7), ti(6), ti(3), A.add)
    ts(ti(0), ti(7), 1023, A.bitwise_and)
    split(7, ti(0), 2, 3)
    tc("v", R("PCB", 192, 576), R("PC", 192, 576))
    late[0] = 0.0
    fill(R("HT", V, V + 32), 0.0)
    for h in range(2):
        o = R("b%d" % (2 + h))
        mm([(o, R("D2"), R("IA", 512 * h, 512 * h + 512), True, False)])
        cell = lambda n, b: R(n, 64 * b, 64 * b + 64)
        mm([(cell("b%d" % (2 + h), b), wr(8 * h + b, k), cell("PCB", i), False, False) for b in range(8) for i, k in enumerate(kinds[:3])])
        mm([(o, R("D3"), R("IB", 512 * h, 512 * h + 512), False, True)])
        tc("v" if h else "s", R("HTP", 512 * h, 512 * h + 512), o)
    for h in range(2):
        o = R("b%d" % h)
        mm([x for b in range(8) for x in [(cell("b%d" % h, b), R("ID"), cell("HTP", 8 * h + b), True, False)] +
            [(cell("b%d" % h, b), wr(8 * h + b, k), cell("PCB", i), False, i == 8) for i, k in enumerate(kinds) if i > 2]])
        tc("s", R("HT", 512 * h, 512 * h + 512), o)
    by(R("HTS"), R("HT"), c1("WC", 8))

    def wcol(j, a, x, b, y):
        if y == 1:
            ts(c1("WC", j), oh(a), float(x), A.mult, oh(b), A.add)
        else:
            ts(c1("WC", 10 + j % 2), oh(b), float(y), A.mult)
            ts(c1("WC", j), oh(a), float(x), A.mult, c1("WC", 10 + j % 2), A.add)
    wcol(0, 0, 8, 1, 1)
    wcol(1, 2, 4, 3, 1)
    wcol(2, 4, -16, 5, -1)
    wcol(3, 7, 4, 8, 1)
    wcol(4, 9, 8, 10, 1)
    wcol(5, 11, 4, 12, 1)
    ts(c1("WC", 6), oh(6), -131072.0, A.mult)
    for n, s in (("BV", oh(6)), ("BE", c1("WC", 0)), ("BA", c1("WC", 1)), ("BSX", c1("WC", 2)), ("BJ", c1("WC", 3)),
                 ("B2", 2.0), ("BM1", -1.0), ("B16", 16.0), ("BHF", 0.5)):
        by(R(n), R("BASE"), s)
    ts(R("CT1", 0, 128), R("C15", 0, 128), PM, A.is_le)
    tt(R("TGE"), R("CT1", 0, 128), R("GSEL"), A.mult)
    ts(R("CT2", 0, 128), R("C15", 0, 128), PM, A.is_gt)
    tt(R("TST"), R("CT2", 0, 128), R("GSEL"), A.mult)
    ts(R("TSN"), R("TST"), -1.0, A.mult)
    for n, s in (("IH", 1.0), ("NIH", -1.0), ("IKH", 1024.0)):
        ts(R(n), R("ID"), s, A.mult)
    for n, s in (("NID", -1.0), ("NIK", -1024.0), ("I8", 8192.0), ("NI8", -8192.0), ("I22", 4194304.0), ("NI22", -4194304.0), ("IKP", c1("WC", 8))):
        by(R(n), R("ID"), s)
    for t in range(RO):
        k = 64 * t
        ts(R("RR", k, k + 64), R("CX", 0, 64), float((64 - ST // 16 * t) % 64), A.add)
        ts(R("CT1", k, k + 64), R("RR", k, k + 64), 63, A.bitwise_and)
        ts(c1("RC", t), c1("PII", 0), float((64 - ST // 16 * t) % 64), A.add)
        ts(c1("RC", 4 + t), c1("RC", t), 63, A.bitwise_and)
        tc("v", c1("RCF", t), c1("RC", 4 + t))
        ts(R("NT", k, k + 64, p=64), R("CT1", k, k + 64, p=64), R("RCF", t, t + 1, p=64), A.is_ge, -1.0, A.mult)
        ts(R("JV", k, k + 64), R("CT1", k, k + 64), 16.0, A.mult, PM, A.add)
        ts(R("JC", k, k + 64), R("JV", k, k + 64), -1.0, A.mult, 1023.0, A.add)
    ts(R("GSELN"), R("GSEL"), -1.0, A.mult)
    tc("v", R("GSELH"), R("GSEL"))
    tc("v", R("BASEH"), R("BASE"))
    for n, s in (("GA", c1("WC", 1)), ("GUU", c1("WC", 4)), ("GAA", c1("WC", 5)), ("GHE", c1("WC", 6)), ("G16", 16.0)):
        by(R(n), R("GSEL"), s)
    tt(R("NEWP", 0, 128), R("GUU"), R("C15", 0, 128), A.mult)
    tt(R("GCT"), R("NEWP", 0, 128), R("GAA"), A.add)
    for j, n in ((0, "PL0"), (1, "PL1")):
        ts(R("CT1", 128 * j, 128 * j + 128), R("C15", 0, 128), float(j), A.is_equal)
        tt(R(n), R("CT1", 128 * j, 128 * j + 128), R("GSEL"), A.mult)
    fill(R("ON"), 1.0)
    fill(R("ONN"), -1.0)
    tc("v", R("MC"), R("C15"))
    ts(R("RST"), R("C15"), 0.0, A.is_equal, 1000000.0, A.mult)
    ts(R("QC", 0, 24), R("CX", 0, 24), 0.0, A.mult, 383.0, A.add)
    ts(R("QC", 24, 48), R("CX", 0, 24), 0.0, A.mult)
    ts(R("QC", 48, 72), R("CX", 0, 24), 16.0, A.mult, PM, A.add)
    q48 = lambda n, a, b: R(n, a, b, p=48)
    ts(q48("QT", 0, 24), q48("CX", 0, 24), q48("PF", 0, 1), A.is_gt, -1.0, A.mult)
    ts(q48("QT", 24, 48), q48("CX", 0, 24), q48("PF", 5, 6), A.is_gt, q48("PF", 4, 5), A.mult)
    tt(q48("RU", 0, 24), q48("QT", 0, 24), q48("QT", 24, 48), A.subtract)
    ts(q48("QT", 48, 72), q48("RU", 0, 24), q48("PF", 4, 5), A.add)
    ts(q48("SC", 0, 1), q48("PF", 4, 5), -1.0, A.mult, 1.0, A.add)
    tc("v", q48("SC", 1, 2), q48("PF", 4, 5))
    ts(R("EQ", 0, 16), R("CX", 0, 16), PM, A.is_le, 4096.0, A.mult)
    ts(R("TG3"), R("OH"), 4096.0, A.mult)
    tt(R("UPM"), R("EQ", 0, 16), R("TG3"), A.add)
    ts(R("CT1", 256, 384), R("C15", 0, 128), 1.0, A.add)
    tt(R("CT2", 256, 384), R("CT1", 256, 384), R("GSEL"), A.mult)
    ts(R("CM"), R("CT2", 256, 384), -1.0, A.add)
    ts(R("G16H"), R("GSEL"), 16.0, A.mult)
    ts(R("JNK"), PM, 1032.0, A.add)
    fill(R("SS", TY, TY + 16), 0.0)
    ts(R("THF"), R("THI"), -1.0, A.mult, -8192.5, A.add)
    tc("v", R("TB"), R("THF"))

    tc("v", R("WD"), R("WDI"))
    send("H", 0, R("HT", 0, V))
    send("X", 0, R("XS"))
    send("W", 0, R("WD"))
    for t in range(1, RO):
        send("X", t, R("XS"))
    for t in range(RO):
        for k, n in (("X", "XE"), ("H", "HE"), ("W", "WE")):
            recv(k, t, R(n, V * t, V * t + V))

    cc = lambda j, m=1: R("CC", NC * j, NC * (j + m))
    for t in range(RO):
        if t:
            send("H", t, R("HT", 0, V))
            send("W", t, R("WD"))
        kt = 64 * t
        at[2] = "L" if t == RO - 1 else ""
        if t == 0:
            chain(R("b5", 0, 64), wrap("BV", "SGA", 0, V))
            tc("v", R("V16"), R("b5", 0, 64))
        else:
            tt(R("V16"), R("V16L"), R("b7", 192, 256), A.is_gt)
        mark("A")
        tt(R("VJ"), R("V16"), R("JC", kt, kt + 64), A.mult)
        chain(R("b6", 0, 128, p=64), [(R("V16"), R("GSEL"))])
        tc("v", R("CT16"), R("b6", 0, 128, p=64))
        chain(R("b5", 0, 64), [(R("IH"), R("JV", kt, kt + 64)), (R("TGE"), R("V16")), (R("IH"), R("VJ")), (R("CT16"), R("NT", kt, kt + 64))])
        tc("v", R("OFF"), R("b5", 0, 64))
        tc("v", X("PERM", 0, V, "OFF", 0, 64), R("HT" if t else "HTP", 0, V))
        chain(R("b6", 0, NC), wrap("BE", "PERM", 0, LN))
        tc("v", R("Y16"), R("b6", 0, NC))
        chain(R("b5", 0, NC), wrap("BA", "PERM", 0, LN))
        tc("v", R("A16"), R("b5", 0, NC))
        for a, b in ((0, 8), (8, NC)):
            tc("v", R("K16", 16 * a, 16 * b), X("RQ", 0, TY, "Y16", a, b))
        for a, b in ((0, 8), (8, NC)):
            tc("v", R("W16", 16 * a, 16 * b), X("WD", 0, V, "A16", a, b))
        mark("Z")
        if t == 0:
            tc("s", R("PERM", 0, LN), X("HT", 0, V, "A16", 0, NC))
        mark("K")
        tc("v", R("KF"), R("K16"))
        tc("v", R("WF"), R("W16"))
        ts(R("DAT"), R("K16"), 2048.0, A.is_ge)
        for k, n in ((7, "IA"), (8, "IB")):
            add("y", lambda g, T, k=k, n=n: g.sync.dma_start(out=T["PERM"][k:128:16, 0:LN], in_=T[n][k:128:16, 0:LN]),
                [R(n, 0, LN)], [R("PERM", 0, LN)], 0.1, kind="dma", sem="ln%d%d" % (k, t), lat=2.5)
        last = t == RO - 1
        if not last:
            add("y", lambda g, T: g.sync.dma_start(out=T["VP"][:, LN:V], in_=T["PERM"][:, LN:V]),
                [R("PERM", LN, V)], [R("VP", LN, V)], 0.1, kind="dma", sem="vp%d" % t, lat=3.0)
        mark("B")
        z, nn = R("b7", 0, NC), R("b2", 0, NC)
        chain(R("b6", 0, 1), [(R("CT16"), R("ON", 0, 1, p=64))])
        ts(R("NX"), R("QC", 48, 72), R("b6", 0, 1), A.add, 1023.5, A.is_gt)
        chain(z, [(R("NIK"), R("NX"))] + wrap("BM1", "DAT", 0, LN), last=False)
        tc("v", R("YI"), R("Y16"))
        hb = lambda j: R("HB", NC * j, NC * j + NC)
        tt(hb(0), R("YI"), R("YI"), A.mult)
        ts(hb(1), hb(0), 4, A.arith_shift_right)
        ts(hb(2), R("YI"), 5.0, A.mult, 8.0, A.add)
        tt(hb(3), hb(1), hb(2), A.add)
        l0 = 0
        for i, L in enumerate(CH):
            l1 = l0 + L
            g0, g1 = 16 * l0, 16 * l1
            E, D = R("b%d" % (i % 2), 0, L), R(("b2", "b3", "b5", "b6")[i % 4], 0, L)
            sl = lambda n: R(n, l0, l1)
            tc("s", R("SGA", g0, g1), X("SS", 0, TY + 16, "K16", l0, l1))
            tc("v" if i in HV else "s", R("HGA", g0, g1), X("HT", 0, V, "W16", l0, l1))
            tt(R("MXA", g0, g1), X("XS", 0, V, "W16", l0, l1), R("SGA", g0, g1), A.max)
            pick = lambda m, n: [(sh(m, p), R(n, g0 + p, g1, 16)) for p in range(16)]
            chain(E, pick("BE", "HGA") + [(R("NIH"), sl("KF"))])
            late[0] = EARLY
            ts(sl("OTB"), E, 0.0, A.not_equal)
            late[0] = 0.0
            chain(D, [(R("NI8"), sl("DAT"))] + pick("BM1", "SGA"), last=False)
            chain(D, pick("BSX", "HGA"), first=False, last=False)
            chain(D, pick("B2", "MXA"), first=False, last=False)
            chain(D, [(R("I8"), sl("OTB"))], first=False)
            act(sl("FB"), D, ActivationFunctionType.Sign, R("TB"))
            chain(R("b4", 0, L), [(R("IH"), sl("WF")), (R("IKH"), sl("KF")), (R("NI22"), sl("DAT")), (R("I22"), sl("OTB"))])
            tc("s", sl("QP"), R("b4", 0, L))
            l0 = l1
        chain(z, wrap("BASE", "OTB", 0, LN), first=False, last=False)
        chain(z, wrap("B16", "FB", 0, LN), first=False)
        chain(nn, wrap("BHF", "FB", 0, LN))
        for j, b in ((1, 1.0), (2, 32.0), (3, 128.0)):
            ts(cc(j), z, b - 256.0, A.is_ge)
        ts(R("OX"), z, -255.0, A.is_lt)
        tt(R("PRO", 0, 48), cc(1, 2), cc(2, 2), A.subtract)
        tt(R("PRO", 48, 72), R("OX"), cc(3), A.add)
        hl = lambda j: R("HL", NC * j, NC * j + NC)
        ts(R("HLV", 48, 72), z, -224.0, A.is_lt)
        mark("C")
        mm([(R("b3", r, LN, 16), wr(r, 6), R("HLV", 48, 72), True, True) for r in range(16)])
        tc("s", R("VP", 0, LN), R("b3", 0, LN))
        if not last:
            tc("s", R("HTV"), X("VP", 0, V, "OFF", 0, 64))
            ts(cc(0), z, -256.0, A.is_ge)
            chain(R("b7", 64, 128), wrap("BV", "HTV", 0, V))
            tc("v", R("V16L"), R("b7", 64, 128))
        mark("D")
        tt(hl(2), nn, hb(3), A.add)
        chain(R("b5", 0, 128, p=48), [(cc(1, 2), R("GSEL")), (cc(2, 2), R("GSELN"))])
        tc("v", R("CP"), R("b5", 0, 128, p=48))
        mm([(R("b6", 0, 72), R("IH"), R("QC"), True, False), (R("b6", 0, 24), R("TSN"), R("PRO", 0, 24), False, False),
            (R("b6", 24, 48), R("TST"), R("PRO", 24, 48), False, False), (R("b6", 48, 72), R("TSN"), R("PRO", 0, 24), False, False),
            (R("b6", 48, 72), R("TSN"), R("PRO", 24, 48), False, False), (R("b6", 0, 72), R("CP"), R("QT"), False, True)])
        tt(R("MU"), R("b6", 0, 72), R("PRO"), A.mult)
        chain(R("b5", 0, NC), [(R("IH"), R("MU", 24 * j, 24 * j + 24)) for j in range(3)])
        tc("v", R("OF2"), R("b5", 0, NC))
        chain(R("b6", 0, 2), [(R("CP"), R("SC"))])
        tc("v", R("PT"), R("b6", 0, 2))
        tc("v", X("P2", 0, LN, "OF2", 0, NC), R("PERM", 0, LN))
        ts(hl(3), hl(2), 2047, A.bitwise_and)
        tt(hl(4), hl(3), R("YI"), A.subtract)
        tt(hl(5), hl(4), cc(3), A.mult)
        tt(hl(2), hl(5), R("YI"), A.add)
        ts(hl(0), hl(2), 3, A.arith_shift_right)
        ts(hl(1), hl(2), 7, A.bitwise_and)
        tc("v", R("HLV", 0, 48), R("HL", 0, 48))
        mm([(R("b4", 0, LN), R("ID"), R("VP", 0, LN), True, False)])
        for r0 in range(0, 16, 8):
            mm([(R("b4", r, LN, 16), wr(r, k), R("HLV", 24 * k, 24 * k + 24), False, False) for r in range(r0, r0 + 8) for k in (0, 1)])
        mm([(R("b4", 0, LN), R("IKP"), R("PERM", 0, LN), False, True)])
        tc("s", R("PERM", 0, LN), R("b4", 0, LN))
        if t:
            tc("s", R("HT", 0, V), X("PERM", 0, V, "OFF", 0, 64))
        else:
            tc("v", X("HT", 0, V, "A16", 0, NC), R("PERM", 0, LN))
        chain(R("b6", 0, NC), wrap("BJ", "P2", 0, LN))
        tc("v", R("JP", 0, 1), R("b6", NC - 1, NC))
        tc("v", R("LJ"), R("b6", 0, NC))
        ts(R("OT"), X("QP", 0, LN, "JP", 0, 1), 4194304.0, A.is_ge)
        tc("v", R("GI"), X("QP", 0, LN, "JP", 0, 1))
        chain(R("b5", 0, 16), [(R("TST"), R("OT"))])
        for j, (s, m) in enumerate(((4, 63), (0, 15), (13, 255), (10, 7))):
            ts(R("WKL", 16 * j, 16 * j + 16), R("GI"), s, A.arith_shift_right, m, A.bitwise_and)
        tt(R("FST"), R("OT"), R("b5", 0, 16), A.is_gt)
        for j in range(4):
            tt(R("PRD", 16 * j, 16 * j + 16), R("FST"), R("WKL", 16 * j, 16 * j + 16), A.mult)
        mark("E")
        if not last:
            chain(R("b6", 0, 2), [(sh("BASEH", r), R("PRD", r, 32, 16)) for r in range(16)])
            ts(R("VLD"), R("PT", 0, 1), PM, A.add, 15.5, A.is_gt)
            ts(R("OHB"), R("CM"), R("b6", 1, 2), A.is_equal)
            ts(R("OHI"), R("CX", 0, 64), R("b6", 0, 1), A.is_equal, R("VLD"), A.mult)
            chain(R("b7", 192, 256), [(R("OHB"), R("OHI"))])
        mark("F")
        chain(R("b5", 0, 16), [(R("IH"), R("UPM")), (R("G16H"), R("PRD", 0, 16)), (R("GSELH"), R("PRD", 16, 32))])
        red(R("TW8"), R("b5", 0, 16), A.max)
        ts(R("EQ", 0, 16), R("b5", 0, 16), 8192.0, A.add, R("TW8"), A.is_equal)
        ts(R("EQ", 16, 17), R("PT", 0, 1), PM, A.add, 15.5, A.is_lt)
        ts(R("TWC"), R("TW8"), -8192.0, A.add)
        red(R("BAD"), R("EQ"), A.max)
        ts(R("TG", 0, 1), R("JNK"), R("BAD"), A.mult, R("TWC"), A.max)
        chain(R("b4", 400, 416), [(R("PL0"), R("PRD", 32, 48)), (R("PL1"), R("PRD", 48, 64))])
        tc("v", R("OKT"), R("b4", 400, 416))
        tt(R("NK"), X("HTS", 0, V + 32, "TG", 0, 1), R("OKT"), A.add)
        tc("v", X("HT", 0, V + 32, "TG", 0, 1), R("NK"))
        late[0] = LATE
        rx = lambda j: R("RX", 48 * j, 48 * j + 48)
        slots = R("P2", 0, SL)
        mm([(R("b0", 0, 48), R("GCT"), slots, True, True)])
        chain(R("b1", 0, 3), wrap("BA", "P2", 0, SL))
        tc("v", rx(0), R("b0", 0, 48))
        tc("v", R("RL", 96, 99), R("b1", 0, 3))
        ts(rx(1), rx(0), 1023, A.bitwise_and)
        tc("v", R("RL", 0, 48), rx(1))
        tc("s", R("XA", 0, 48), X("XS", 0, V, "RL", 96, 99))
        for h in range(2):
            a, b = 384 * h, 384 * h + 384
            o = R("b%d" % (2 + h), 0, 384)
            q = "v" if last and h == 0 else "s"
            tc(q, R("MX", a, b), X("XE", V * t, V * t + V, "RL", 24 * h, 24 * h + 24))
            tc(q, R("HEG", a, b), X("HE", V * t, V * t + V, "RL", 24 * h, 24 * h + 24))
            mm([x for m in range(16) for x in ((R(o[1], m, 384, 16), R("NID"), R("XA", 24 * h, 24 * h + 24), True, False),
                                               (R(o[1], m, 384, 16), R("ID"), R("MX", a + m, b, 16), False, True))])
            act(R("GAB", a, b), o, ActivationFunctionType.Abs)
        rb = lambda j: R("RB", 48 * j, 48 * j + 48)
        rf = lambda j: R("RF", 48 * j, 48 * j + 48)
        act(rb(0), X("FB", 0, LN, "LJ", 0, 3), ActivationFunctionType.Relu)
        ts(rb(1), R("CX", 0, 48), R("PT", 1, 2), A.is_lt)
        tt(rb(2), rb(0), rb(1), A.mult)
        tc("v", rf(0), X("WD", 0, V, "RL", 96, 99))
        for h in range(2):
            a, b = 384 * h, 384 * h + 384
            o = R("b%d" % (2 + h), 0, 384)
            chain(o, [(R("ID"), R("MC")), (R("GHE"), R("HEG", a, b)), (R("G16"), R("GAB", a, b))])
            scan(R("KS", a, b), R("RST"), o, 1000000.0, A.add, A.min)
        late[0] = LATE2
        key = R("KS", 15, 768, 16)
        ts(rx(3), key, 15, A.bitwise_and)
        ts(rb(3), rx(3), PM, A.is_equal)
        tt(R("RH"), rb(3), rx(1), A.mult)
        chain(R("b1", 0, 3), [(sh("BASEH", r), R("RH", r, 48, 16)) for r in range(16)])
        tc("v", R("RL", 100, 103), R("b1", 0, 3))
        ts(rb(0), key, 0.0, A.is_lt)
        tt(rb(1), rb(0), rb(2), A.mult)
        tt(rf(1), rf(0), rb(1), A.mult)
        tt(rf(2), rf(0), rf(1), A.subtract)
        tt(rf(3), X("WE", V * t, V * t + V, "RL", 100, 103), rb(1), A.mult)
        tt(X("WD", 0, V, "RL", 96, 99), rf(3), rf(2), A.add)
        late[0] = 0.0
        mark("G")
        if not last:
            chain(R("b1", 0, NC), [(R("ON"), cc(0)), (R("ONN"), cc(2))])
            red(R("BS"), R("b1", 0, NC), A.add)
            tc("v", R("BI", 0, 1), R("BS"))
            ts(R("BI", 1, 2), R("BI", 0, 1), 255, A.bitwise_and)
            ts(R("TB"), R("BI", 1, 2), -1.0, A.mult, R("THF"), A.add)
    store("y", "ym", R("WD"), "oym")
    for j, m in ((0, "WC0"), (1, "OH6")):
        ts(R("EQ", 8 * j, 8 * j + 8), R("CX", 0, 8), PG, A.is_equal)
        ts(R("NEWP", 8 * j, 8 * j + 8), R("EQ", 8 * j, 8 * j + 8), c1("WC", 0) if j == 0 else oh(6), A.mult)
        for h in range(2):
            o = R("b%d" % (4 + 2 * j + h), 0, 512, p=8)
            chain(o, [(R("NEWP", 8 * j, 8 * j + 8), R("HT", 512 * h, 512 * h + 512))])
            tc("v" if h else "s", R("Y8", V * j + 512 * h, V * j + 512 * h + 512), o)
        store("y", "yh" if j == 0 else "yv", R("Y8", V * j, V * j + V), "oyh" if j == 0 else "oyv")
    return ops


def link(ops):
    seen = {}
    for j, o in enumerate(ops):
        deps = {}

        def need(i, w):
            deps[i] = deps.get(i, False) or w
        for wrt, regs in ((False, o["rd"]), (True, o["wr"])):
            for n, a, b in regs:
                bank = SCRATCH[n][0] == "psum"
                for (i, ia, ib, iw) in seen.get(n, []):
                    if i == j:
                        continue
                    same = ops[i]["q"] == o["q"] and o.get("kind") is None and ops[i].get("kind") is None
                    over = ia < b and a < ib
                    if over and (wrt or iw):
                        if same:
                            need(i, o["q"] != "t")
                        else:
                            need(i, True)
                    elif bank:
                        need(i, not same)
        for wrt, regs in ((False, o["rd"]), (True, o["wr"])):
            for n, a, b in regs:
                lst = seen.setdefault(n, [])
                if wrt:
                    bank = SCRATCH[n][0] == "psum"
                    lst[:] = [e for e in lst if e[0] == j or not (a <= e[1] and e[2] <= b)]
                lst.append((j, a, b, wrt))
        o["deps"] = deps
    return ops


def order(ops):
    n = len(ops)
    nxt = [[] for _ in range(n)]
    for j, o in enumerate(ops):
        for i in o["deps"]:
            nxt[i].append(j)
    rank = [0.0] * n
    for i in range(n - 1, -1, -1):
        best = 0.0
        for j in nxt[i]:
            best = max(best, rank[j] + (WAKE if ops[j]["deps"][i] else 0.0))
        rank[i] = ops[i]["cost"] + ops[i]["lat"] + best
    def own(k):
        return PRIO.get(k, PRIO.get(k[1:], 0.0) if k[0] == "L" else 0.0)
    rank = [x - ops[i]["late"] + own(ops[i]["key"]) for i, x in enumerate(rank)]
    left = [len(o["deps"]) for o in ops]
    ready = [0.0] * n
    pend = {}
    for i, o in enumerate(ops):
        if left[i] == 0:
            pend.setdefault(o["q"], []).append(i)
    free = {}
    seq = []
    while len(seq) < n:
        pick = None
        for q, lst in pend.items():
            if not lst:
                continue
            f = free.get(q, 0.0) if q is not None else 0.0
            s = min(max(f, ready[i]) for i in lst)
            best = max((i for i in lst if max(f, ready[i]) <= s + 0.04), key=lambda i: rank[i])
            s = max(f, ready[best])
            if pick is None or s < pick[0]:
                pick = (s, q, best)
        s, q, i = pick
        pend[q].remove(i)
        o = ops[i]
        o["start"] = s
        end = s + o["cost"]
        free[q] = end
        seq.append(i)
        for j in nxt[i]:
            e = ops[j]["deps"][i]
            ready[j] = max(ready[j], end + o["lat"] + WAKE if e else s)
            left[j] -= 1
            if left[j] == 0:
                pend.setdefault(ops[j]["q"], []).append(j)
    return seq


QSEM = {"v": "sv", "s": "ss", "t": "st", "g": "sg"}


def waits(ops, seq):
    for o in ops:
        o["sig"] = False
    for o in ops:
        for i, w in o["deps"].items():
            if w:
                ops[i]["sig"] = True
    count, know, value = {}, {}, {}
    total = {}
    for i in seq:
        o = ops[i]
        q = o["q"]
        k = know.setdefault(q, {}) if q is not None else {}
        wl = {}
        for d in sorted(o["deps"], key=lambda d: -ops[d]["start"]):
            if not o["deps"][d]:
                continue
            sem, val = value[d]
            if k.get(sem, 0) >= val:
                continue
            wl[sem] = max(wl.get(sem, 0), val)
            k[sem] = max(k.get(sem, 0), val)
            for s2, v2 in ops[d]["knows"].items():
                k[s2] = max(k.get(s2, 0), v2)
        o["waits"] = wl
        o["knows"] = dict(k)
        if o.get("kind") is not None:
            value[i] = (o["sem"], 1)
            total[o["sem"]] = 1
        elif o["sig"]:
            sem = QSEM[q]
            count[sem] = count.get(sem, 0) + o["incs"]
            value[i] = (sem, count[sem])
            total[sem] = count[sem]
        if i in value:
            o["knows"][value[i][0]] = value[i][1]
    return total


PLAN = {}


def plan():
    if not PLAN:
        ops = link(make_program())
        seq = order(ops)
        PLAN["ops"], PLAN["seq"], PLAN["total"] = ops, seq, waits(ops, seq)
    return PLAN["ops"], PLAN["seq"], PLAN["total"]


def rank_program(g, core, T, topo):
    rank = T.rank_of(core)
    if rank is None:
        return
    ops, seq, total = plan()
    queue = {"v": g.vector, "s": g.scalar, "t": g.tensor, "g": g, "y": g.sync}

    def full(sem, val):
        if sem in ("sv", "ss", "st", "sg"):
            return val
        if sem[:2] in ("ld", "vp", "ln") or sem[0] == "o":
            return 16
        t = int(sem[4])
        if sem[:3] == "arr":
            src = T.cores[(rank + 1 + t) % N]
            return len(topo.engines(src, core))
        return len(topo.engines(core, T.cores[(rank - 1 - t) % N]))

    for i in seq:
        o = ops[i]
        if o["q"] is None:
            continue
        for sem in o["waits"]:
            queue[o["q"]].wait_ge(T.sem[sem], full(sem, o["waits"][sem]))
        kind = o.get("kind")
        if kind == "send":
            k, t, src = o["call"]
            dst = T.cores[(rank - 1 - t) % N]
            rid, pid, _ = topo.addr(dst)
            g.remote_dma(ap(T, R({"X": "XE", "H": "HE", "W": "WE"}[k], V * t, V * t + V)), ap(T, src),
                         T.sem["arr%s%d" % (k, t)], T.sem["loc%s%d" % (k, t)], pid, rid, topo.mask(core, dst))
        elif kind == "dma":
            o["call"](g, T).then_inc(T.sem[o["sem"]], 16)
        elif o["q"] == "t":
            o["call"](g, T, T.sem["st"] if o["sig"] else None)
        else:
            c = o["call"](g, T)
            if o["sig"]:
                c.then_inc(T.sem[QSEM[o["q"]]], 1)
    for sem in total:
        g.wait_ge(T.sem[sem], full(sem, total[sem]))
